import numpy as np
import ml_dtypes


def mxq(x, axis, fmt="e4m3"):
    dtype, down = {"e4m3": (ml_dtypes.float8_e4m3fn, 7), "e5m2": (ml_dtypes.float8_e5m2, 14)}[fmt]
    v = np.moveaxis(np.asarray(x, np.float32).astype(ml_dtypes.bfloat16).astype(np.float64), axis, -1)
    blocks = v.reshape(v.shape[:-1] + (-1, 32))
    amax = np.abs(blocks).max(-1, keepdims=True)
    byte = np.maximum(np.where(amax > 0, np.frexp(amax)[1] - 1 + 127, 0) - down, 1)
    scale = np.exp2(byte - 127.0)
    codes = (blocks / scale).astype(np.float32).astype(dtype).astype(np.float64)
    return np.moveaxis((codes * scale).reshape(v.shape), -1, axis)


WIDE = False


def mx_kscale(k):
    if not WIDE:
        return np.ones(k)
    levels = np.array([30, -30])
    if k % 512:
        return np.exp2(np.random.permutation(np.resize(levels, k // 32))).repeat(32)
    a = np.empty((k // 512, 16))
    for p in range(k // 512):
        a[p, :8] = np.random.permutation(np.resize(levels, 8))
        for g in range(8):
            far = levels[np.abs(levels - a[p, g]) >= 10]
            a[p, g + 8] = far[np.random.randint(len(far))]
    return np.exp2(a.ravel()).repeat(32)


def f64(x):
    return np.asarray(x).astype(np.float64)


E2M1 = np.array([0.0, 0.5, 1.0, 1.5, 2.0, 3.0, 4.0, 6.0, -0.0, -0.5, -1.0, -1.5, -2.0, -3.0, -4.0, -6.0])


def pack_weight(w, fmt):
    k, n = w.shape
    w = f64(np.asarray(w, np.float32).astype(ml_dtypes.bfloat16)).reshape(k // 32, 32, n)
    amax = np.abs(w).max(1)
    if fmt == "e4m3":
        byte = np.frexp(amax)[1] - 1 + 127 - 7
    else:
        mant, ex = np.frexp(amax / 6.0)
        byte = np.where(mant > 0.5, ex, ex - 1) + 127
    byte = np.clip(np.where(amax > 0, byte, 1), 1, 254)
    scaled = (w * np.exp2(127.0 - byte)[:, None, :]).reshape(k, n).astype(np.float32)
    by_word = np.ascontiguousarray(scaled.reshape(k // 512, 128, 4, n).transpose(0, 1, 3, 2))
    if fmt == "e4m3":
        words = by_word.astype(ml_dtypes.float8_e4m3fn).view(np.uint8)
    else:
        c = by_word.astype(ml_dtypes.float4_e2m1fn).view(np.uint8) & 0xF
        words = (c[..., 0::2] | (c[..., 1::2] << 4)).reshape(k // 512, 128, 2 * n)
    return np.ascontiguousarray(words), np.ascontiguousarray(byte.astype(np.uint8).reshape(k // 512, 16, n))


def unpack_weight(words, scales, fmt):
    g, _, n = scales.shape
    words = np.ascontiguousarray(words).reshape(g, 128, n, -1)
    if fmt == "e4m3":
        vals = words.view(ml_dtypes.float8_e4m3fn).astype(np.float64)
    else:
        nib = np.empty((g, 128, n, 4), np.uint8)
        nib[..., 0::2] = words & 0xF
        nib[..., 1::2] = words >> 4
        vals = E2M1[nib]
    vals = vals * np.repeat(np.exp2(scales.astype(np.float64) - 127.0), 8, axis=1)[..., None]
    return vals.transpose(0, 1, 3, 2).reshape(g * 512, n)


K, L, M, N = 1024, 1024, 1024, 1024


def setup_inputs():
    n = np.random.standard_normal
    s = mx_kscale(K)[:, None]
    u = mx_kscale(L)[:, None]
    p_am = pack_weight(n((K, M)) / s, "e2m1")
    p_bm = pack_weight(n((L, N)) / np.sqrt(L) / u, "e2m1")
    return {
        "g": (n((K, L)) / np.sqrt(K) * s * u.T).astype(np.float32),
        "am_words": p_am[0],
        "am_scales": p_am[1],
        "bm_words": p_bm[0],
        "bm_scales": p_bm[1],
        "mom": (n((M, N))).astype(np.float32),
    }


def reference(g, am_words, am_scales, bm_words, bm_scales, mom):
    g_ = mxq(f64(g), 0, "e5m2")
    am_ = unpack_weight(am_words, am_scales, "e2m1")
    h = g_.T @ am_
    h_ = mxq(h, 0, "e4m3")
    bm_ = unpack_weight(bm_words, bm_scales, "e2m1")
    y = h_.T @ bm_
    return 0.9 * f64(mom) + y

@@ -1,0 +1,239 @@
+from contextlib import ExitStack
+
+import concourse.mybir as mybir
+
+K, L, M, N = 1024, 1024, 1024, 1024
+FLOPS = 2 * K * L * M + 2 * L * M * N
+
+F32 = mybir.dt.float32
+BF16 = mybir.dt.bfloat16
+I32 = mybir.dt.int32
+U32 = mybir.dt.uint32
+U8 = mybir.dt.uint8
+E5M2X4 = mybir.dt.float8_e5m2_x4
+E4M3X4 = mybir.dt.float8_e4m3fn_x4
+E2M1X4 = mybir.dt.float4_e2m1fn_x4
+
+P = 128
+PACK = 4
+SPAN = P * PACK
+BANKS = 8
+DECAY = 0.9
+G_VECTOR_SHARE = 80
+
+
+def tile_mix_kfac_ema_kernel(tc, g, am_words, am_scales, bm_words, bm_scales, mom, out):
+    nc = tc.nc
+    with ExitStack() as ctx:
+        sb = ctx.enter_context(tc.tile_pool(name="sb", bufs=1))
+        psum = ctx.enter_context(tc.psum_pool(name="psum", bufs=1))
+        ctx.enter_context(tc.manual_schedule())
+
+        def sbuf(name, shape, dtype):
+            return sb.tile(shape, dtype, name=name, align_bytes=64)
+
+        def bank(index):
+            return psum.tile([P, SPAN], F32, name="acc", tag="bank%d" % index)
+
+        am_plane = sbuf("am_plane", [P, 2, M], U8)
+        bm_plane = sbuf("bm_plane", [P, 2, N], U8)
+        nc.vector.memset(am_plane[:].bitcast(I32), 0)
+        nc.vector.memset(bm_plane[:].bitcast(I32), 0)
+
+        def load_plane(plane, scales):
+            rows = scales.rearrange("a (quad r) c -> r quad a c", r=4)
+            for r in range(4):
+                nc.sync.dma_start(out=plane[r:P:32, :, :].bitcast(I32), in_=rows[r].bitcast(I32))
+
+        g_raw = {}
+
+        def load_g(b, a):
+            g_raw[b, a] = sbuf("g_raw%d%d" % (b, a), [P, PACK, SPAN], F32)
+            rows = g[a * SPAN : (a + 1) * SPAN, b * SPAN : (b + 1) * SPAN]
+            nc.sync.dma_start(out=g_raw[b, a][:], in_=rows.rearrange("(p j) l -> p j l", j=PACK))
+
+        am_codes = {}
+
+        def load_am(a):
+            am_codes[a] = sbuf("am_codes%d" % a, [P, 2 * M], U8)
+            nc.sync.dma_start(out=am_codes[a][:].bitcast(I32), in_=am_words[a].bitcast(I32))
+
+        load_am(0)
+        load_g(0, 0)
+        load_plane(am_plane, am_scales)
+        load_g(0, 1)
+        load_am(1)
+        load_g(1, 0)
+        load_g(1, 1)
+        bm_codes = sbuf("bm_codes", [P, 2, 2 * N], U8)
+        nc.sync.dma_start(out=bm_codes[:].bitcast(I32), in_=bm_words.rearrange("a p c -> p a c").bitcast(I32))
+        load_plane(bm_plane, bm_scales)
+        mom_sb = {}
+        for half in range(2):
+            rows = mom[half * SPAN : (half + 1) * SPAN, :].rearrange("(q e) n -> q e n", e=PACK)
+            for pair in range(2):
+                mom_sb[half, pair] = sbuf("mom%d%d" % (half, pair), [P, 2, N], F32)
+                nc.sync.dma_start(out=mom_sb[half, pair][:], in_=rows[:, 2 * pair : 2 * pair + 2, :])
+
+        g_codes = {}
+        g_plane = {}
+
+        def quantize_g(b, a, vector_share):
+            grouped = sbuf("g_grouped%d%d" % (b, a), [P, PACK * SPAN], BF16)
+            dst = grouped[:].rearrange("p (t q j) -> p q j t", t=PACK, j=PACK)
+            src = g_raw[b, a][:].rearrange("p j (q t) -> p q j t", t=PACK)
+            nc.vector.tensor_copy(out=dst[:, :vector_share], in_=src[:, :vector_share])
+            if vector_share < P:
+                nc.scalar.copy(out=dst[:, vector_share:], in_=src[:, vector_share:])
+            for pair in range(2):
+                codes = sbuf("g_codes%d%d%d" % (b, a, pair), [P, 2 * P], U32)
+                plane = sbuf("g_plane%d%d%d" % (b, a, pair), [P, 2 * P], U8)
+                nc.vector.quantize_mx(
+                    out=codes[:].bitcast(E5M2X4),
+                    scales=plane[:],
+                    in_=grouped[:, pair * 2 * SPAN : (pair + 1) * 2 * SPAN],
+                )
+                for u in range(2):
+                    g_codes[b, a, 2 * pair + u] = codes[:, u * P : (u + 1) * P]
+                    g_plane[b, a, 2 * pair + u] = plane[:, u * P : (u + 1) * P]
+
+        h_acc = {}
+
+        def multiply_h(b, a, half):
+            for t in range(PACK):
+                if a == 0:
+                    h_acc[b, half, t] = bank(PACK * half + t)
+                nc.tensor.matmul_mx(
+                    out=h_acc[b, half, t][:],
+                    lhsT=g_codes[b, a, t].bitcast(E5M2X4),
+                    lhsT_scale=g_plane[b, a, t],
+                    rhs=am_codes[a][:, half * 2 * SPAN : (half + 1) * 2 * SPAN].bitcast(E2M1X4),
+                    rhs_scale=am_plane[:, a, half * SPAN : (half + 1) * SPAN],
+                    start=(a == 0),
+                    stop=(a == 1),
+                )
+
+        h_rows = {}
+
+        def drain_h(b, half, t, on_vector):
+            if t == 0:
+                h_rows[b, half] = sbuf("h_rows%d%d" % (b, half), [P, PACK, SPAN], BF16)
+            dst = h_rows[b, half][:, t, :].rearrange("p (e q) -> p e q", e=PACK)
+            src = h_acc[b, half, t][:].rearrange("p (q e) -> p e q", e=PACK)
+            if on_vector:
+                nc.vector.tensor_copy(out=dst, in_=src)
+            else:
+                nc.scalar.copy(out=dst, in_=src)
+
+        h_grouped = {}
+
+        def interleave_h(b, half, pair, on_vector):
+            h_grouped[b, half, pair] = sbuf("h_grouped%d%d%d" % (b, half, pair), [P, 2 * SPAN], BF16)
+            dst = h_grouped[b, half, pair][:].rearrange("p (c i t) -> p c t i", i=4, t=PACK)
+            src = h_rows[b, half][:, :, pair * 2 * P : (pair + 1) * 2 * P].rearrange("p t (c i) -> p c t i", i=4)
+            if on_vector:
+                nc.vector.tensor_copy(out=dst, in_=src)
+            else:
+                nc.scalar.copy(out=dst, in_=src)
+
+        h_codes = {}
+        h_plane = {}
+
+        def quantize_h(b, half, pair):
+            h_codes[b, half, pair] = sbuf("h_codes%d%d%d" % (b, half, pair), [P, 2 * P], U32)
+            h_plane[b, half, pair] = sbuf("h_plane%d%d%d" % (b, half, pair), [P, 2 * P], U8)
+            nc.vector.quantize_mx(
+                out=h_codes[b, half, pair][:].bitcast(E4M3X4),
+                scales=h_plane[b, half, pair][:],
+                in_=h_grouped[b, half, pair][:],
+            )
+
+        y_acc = {}
+
+        def multiply_y(tile, side, b):
+            half, e = divmod(tile, PACK)
+            pair, u = divmod(e, 2)
+            if b == 0:
+                y_acc[tile, side] = bank((2 * tile + side) % BANKS)
+            nc.tensor.matmul_mx(
+                out=y_acc[tile, side][:],
+                lhsT=h_codes[b, half, pair][:, u * P : (u + 1) * P].bitcast(E4M3X4),
+                lhsT_scale=h_plane[b, half, pair][:, u * P : (u + 1) * P],
+                rhs=bm_codes[:, b, side * 2 * SPAN : (side + 1) * 2 * SPAN].bitcast(E2M1X4),
+                rhs_scale=bm_plane[:, b, side * SPAN : (side + 1) * SPAN],
+                start=(b == 0),
+                stop=(b == 1),
+            )
+
+        def multiply_tile(tile):
+            for side in range(2):
+                for b in range(2):
+                    multiply_y(tile, side, b)
+
+        def finish(tile):
+            half, e = divmod(tile, PACK)
+            pair, u = divmod(e, 2)
+            result = sbuf("result%d" % tile, [P, N], F32)
+            for side in range(2):
+                cols = slice(side * SPAN, (side + 1) * SPAN)
+                nc.vector.scalar_tensor_tensor(
+                    out=result[:, cols],
+                    in0=mom_sb[half, pair][:, u, cols],
+                    scalar=DECAY,
+                    in1=y_acc[tile, side][:],
+                    op0=mybir.AluOpType.mult,
+                    op1=mybir.AluOpType.add,
+                )
+            rows = out[half * SPAN : (half + 1) * SPAN, :].rearrange("(q e) n -> q e n", e=PACK)
+            nc.sync.dma_start(out=rows[:, e, :], in_=result[:])
+
+        for a in range(2):
+            quantize_g(0, a, G_VECTOR_SHARE)
+            for half in range(2):
+                multiply_h(0, a, half)
+        for half in range(2):
+            for t in range(PACK):
+                drain_h(0, half, t, False)
+        for a in range(2):
+            quantize_g(1, a, P)
+            for half in range(2):
+                multiply_h(1, a, half)
+
+        for pair in range(2):
+            interleave_h(0, 0, pair, True)
+        for pair in range(2):
+            quantize_h(0, 0, pair)
+        for t in range(PACK):
+            drain_h(1, 0, t, t == PACK - 1)
+        for tile in range(2):
+            for side in range(2):
+                multiply_y(tile, side, 0)
+        for t in range(PACK):
+            drain_h(1, 1, t, False)
+        for pair in range(2):
+            interleave_h(1, 0, pair, True)
+        for pair in range(2):
+            quantize_h(1, 0, pair)
+        for tile in range(2):
+            for side in range(2):
+                multiply_y(tile, side, 1)
+        multiply_tile(2)
+        multiply_tile(3)
+        for pair in range(2):
+            for b in range(2):
+                interleave_h(b, 1, pair, False)
+
+        finish(0)
+        finish(1)
+        for b in range(2):
+            quantize_h(b, 1, 0)
+        multiply_tile(4)
+        multiply_tile(5)
+        finish(2)
+        finish(3)
+        for b in range(2):
+            quantize_h(b, 1, 1)
+        multiply_tile(6)
+        multiply_tile(7)
+        for tile in range(4, 8):
+            finish(tile)

@@ -58,8 +58,8 @@ def tile_mix_kfac_ema_kernel(tc, g, am_words, am_scales, bm_words, bm_scales, mo
             am_codes[a] = sbuf("am_codes%d" % a, [P, 2 * M], U8)
             nc.sync.dma_start(out=am_codes[a][:].bitcast(I32), in_=am_words[a].bitcast(I32))
 
-        load_am(0)
         load_g(0, 0)
+        load_am(0)
         load_plane(am_plane, am_scales)
         load_g(0, 1)
         load_am(1)
@@ -78,13 +78,20 @@ def tile_mix_kfac_ema_kernel(tc, g, am_words, am_scales, bm_words, bm_scales, mo
         g_codes = {}
         g_plane = {}
 
-        def quantize_g(b, a, vector_share):
+        g_grouped = {}
+
+        def interleave_g(b, a, vector_share):
             grouped = sbuf("g_grouped%d%d" % (b, a), [P, PACK * SPAN], BF16)
+            g_grouped[b, a] = grouped
             dst = grouped[:].rearrange("p (t q j) -> p q j t", t=PACK, j=PACK)
             src = g_raw[b, a][:].rearrange("p j (q t) -> p q j t", t=PACK)
-            nc.vector.tensor_copy(out=dst[:, :vector_share], in_=src[:, :vector_share])
+            if vector_share > 0:
+                nc.vector.tensor_copy(out=dst[:, :vector_share], in_=src[:, :vector_share])
             if vector_share < P:
                 nc.scalar.copy(out=dst[:, vector_share:], in_=src[:, vector_share:])
+
+        def quantize_g(b, a):
+            grouped = g_grouped[b, a]
             for pair in range(2):
                 codes = sbuf("g_codes%d%d%d" % (b, a, pair), [P, 2 * P], U32)
                 plane = sbuf("g_plane%d%d%d" % (b, a, pair), [P, 2 * P], U8)
@@ -99,8 +106,8 @@ def tile_mix_kfac_ema_kernel(tc, g, am_words, am_scales, bm_words, bm_scales, mo
 
         h_acc = {}
 
-        def multiply_h(b, a, half):
-            for t in range(PACK):
+        def multiply_h(b, a, half, slots=range(PACK)):
+            for t in slots:
                 if a == 0:
                     h_acc[b, half, t] = bank(PACK * half + t)
                 nc.tensor.matmul_mx(
@@ -170,70 +177,87 @@ def tile_mix_kfac_ema_kernel(tc, g, am_words, am_scales, bm_words, bm_scales, mo
                 for b in range(2):
                     multiply_y(tile, side, b)
 
+        result = {}
+
         def finish(tile):
             half, e = divmod(tile, PACK)
             pair, u = divmod(e, 2)
-            result = sbuf("result%d" % tile, [P, N], F32)
+            if u == 0:
+                result[half, pair] = sbuf("result%d%d" % (half, pair), [P, 2, N], F32)
+            rows = out[half * SPAN : (half + 1) * SPAN, :].rearrange("(q e) n -> q e n", e=PACK)
             for side in range(2):
                 cols = slice(side * SPAN, (side + 1) * SPAN)
                 nc.vector.scalar_tensor_tensor(
-                    out=result[:, cols],
+                    out=result[half, pair][:, u, cols],
                     in0=mom_sb[half, pair][:, u, cols],
                     scalar=DECAY,
                     in1=y_acc[tile, side][:],
                     op0=mybir.AluOpType.mult,
                     op1=mybir.AluOpType.add,
                 )
-            rows = out[half * SPAN : (half + 1) * SPAN, :].rearrange("(q e) n -> q e n", e=PACK)
-            nc.sync.dma_start(out=rows[:, e, :], in_=result[:])
+                if tile == 7:
+                    nc.sync.dma_start(out=rows[:, e, cols], in_=result[half, pair][:, u, cols])
+            if tile < 7:
+                nc.sync.dma_start(out=rows[:, e, :], in_=result[half, pair][:, u, :])
 
-        for a in range(2):
-            quantize_g(0, a, G_VECTOR_SHARE)
-            for half in range(2):
-                multiply_h(0, a, half)
-        for half in range(2):
-            for t in range(PACK):
-                drain_h(0, half, t, False)
-        for a in range(2):
-            quantize_g(1, a, P)
-            for half in range(2):
-                multiply_h(1, a, half)
-
-        for pair in range(2):
-            interleave_h(0, 0, pair, True)
-        for pair in range(2):
-            quantize_h(0, 0, pair)
+        interleave_g(0, 0, 84)
+        quantize_g(0, 0)
+        multiply_h(0, 0, 0)
+        multiply_h(0, 0, 1, range(2))
+        interleave_g(0, 1, 84)
+        quantize_g(0, 1)
+        multiply_h(0, 1, 0)
+        multiply_h(0, 0, 1, range(2, 4))
+        multiply_h(0, 1, 1)
         for t in range(PACK):
-            drain_h(1, 0, t, t == PACK - 1)
+            drain_h(0, 0, t, t == 1)
+        for t in range(PACK):
+            drain_h(0, 1, t, False)
+        interleave_g(1, 0, P)
+        interleave_h(0, 0, 0, True)
+        quantize_g(1, 0)
+        multiply_h(1, 0, 0)
+        multiply_h(1, 0, 1, range(2))
+        interleave_g(1, 1, 96)
+        quantize_h(0, 0, 0)
+        quantize_g(1, 1)
+        multiply_h(1, 1, 0)
+        multiply_h(1, 0, 1, range(2, 4))
+        interleave_h(0, 1, 0, False)
+        interleave_h(0, 0, 1, True)
+        for t in range(PACK):
+            drain_h(1, 0, t, t % 2 == 1)
+        quantize_h(0, 0, 1)
+        multiply_h(1, 1, 1)
         for tile in range(2):
             for side in range(2):
                 multiply_y(tile, side, 0)
-        for t in range(PACK):
-            drain_h(1, 1, t, False)
-        for pair in range(2):
-            interleave_h(1, 0, pair, True)
-        for pair in range(2):
-            quantize_h(1, 0, pair)
+        interleave_h(1, 0, 0, True)
+        interleave_h(1, 0, 1, False)
+        quantize_h(0, 1, 0)
+        quantize_h(1, 0, 0)
         for tile in range(2):
             for side in range(2):
                 multiply_y(tile, side, 1)
+        for t in range(PACK):
+            drain_h(1, 1, t, False)
+        quantize_h(1, 0, 1)
         multiply_tile(2)
         multiply_tile(3)
-        for pair in range(2):
-            for b in range(2):
-                interleave_h(b, 1, pair, False)
-
+        interleave_h(1, 1, 0, False)
+        for b in range(2):
+            interleave_h(b, 1, 1, False)
         finish(0)
         finish(1)
-        for b in range(2):
-            quantize_h(b, 1, 0)
+        finish(2)
+        quantize_h(1, 1, 0)
         multiply_tile(4)
         multiply_tile(5)
-        finish(2)
         finish(3)
+        finish(4)
         for b in range(2):
             quantize_h(b, 1, 1)
         multiply_tile(6)
         multiply_tile(7)
-        for tile in range(4, 8):
+        for tile in range(5, 8):
             finish(tile)

@@ -70,10 +70,11 @@ def tile_mix_kfac_ema_kernel(tc, g, am_words, am_scales, bm_words, bm_scales, mo
         load_plane(bm_plane, bm_scales)
         mom_sb = {}
         for half in range(2):
-            rows = mom[half * SPAN : (half + 1) * SPAN, :].rearrange("(q e) n -> q e n", e=PACK)
             for pair in range(2):
+                first = half * SPAN + pair * 2 * P
+                rows = mom[first : first + 2 * P, :].rearrange("(q u) n -> q u n", u=2)
                 mom_sb[half, pair] = sbuf("mom%d%d" % (half, pair), [P, 2, N], F32)
-                nc.sync.dma_start(out=mom_sb[half, pair][:], in_=rows[:, 2 * pair : 2 * pair + 2, :])
+                nc.sync.dma_start(out=mom_sb[half, pair][:], in_=rows)
 
         g_codes = {}
         g_plane = {}
@@ -125,8 +126,8 @@ def tile_mix_kfac_ema_kernel(tc, g, am_words, am_scales, bm_words, bm_scales, mo
         def drain_h(b, half, t, on_vector):
             if t == 0:
                 h_rows[b, half] = sbuf("h_rows%d%d" % (b, half), [P, PACK, SPAN], BF16)
-            dst = h_rows[b, half][:, t, :].rearrange("p (e q) -> p e q", e=PACK)
-            src = h_acc[b, half, t][:].rearrange("p (q e) -> p e q", e=PACK)
+            dst = h_rows[b, half][:, t, :]
+            src = h_acc[b, half, t][:]
             if on_vector:
                 nc.vector.tensor_copy(out=dst, in_=src)
             else:
@@ -136,8 +137,8 @@ def tile_mix_kfac_ema_kernel(tc, g, am_words, am_scales, bm_words, bm_scales, mo
 
         def interleave_h(b, half, pair, on_vector):
             h_grouped[b, half, pair] = sbuf("h_grouped%d%d%d" % (b, half, pair), [P, 2 * SPAN], BF16)
-            dst = h_grouped[b, half, pair][:].rearrange("p (c i t) -> p c t i", i=4, t=PACK)
-            src = h_rows[b, half][:, :, pair * 2 * P : (pair + 1) * 2 * P].rearrange("p t (c i) -> p c t i", i=4)
+            dst = h_grouped[b, half, pair][:].rearrange("p (u c i t) -> p c t i u", u=2, i=2, t=PACK)
+            src = h_rows[b, half][:, :, pair * 2 * P : (pair + 1) * 2 * P].rearrange("p t (c i u) -> p c t i u", i=2, u=2)
             if on_vector:
                 nc.vector.tensor_copy(out=dst, in_=src)
             else:
@@ -184,7 +185,8 @@ def tile_mix_kfac_ema_kernel(tc, g, am_words, am_scales, bm_words, bm_scales, mo
             pair, u = divmod(e, 2)
             if u == 0:
                 result[half, pair] = sbuf("result%d%d" % (half, pair), [P, 2, N], F32)
-            rows = out[half * SPAN : (half + 1) * SPAN, :].rearrange("(q e) n -> q e n", e=PACK)
+            first = half * SPAN + pair * 2 * P
+            rows = out[first : first + 2 * P, :].rearrange("(q u) n -> q u n", u=2)
             for side in range(2):
                 cols = slice(side * SPAN, (side + 1) * SPAN)
                 nc.vector.scalar_tensor_tensor(
@@ -196,9 +198,9 @@ def tile_mix_kfac_ema_kernel(tc, g, am_words, am_scales, bm_words, bm_scales, mo
                     op1=mybir.AluOpType.add,
                 )
                 if tile == 7:
-                    nc.sync.dma_start(out=rows[:, e, cols], in_=result[half, pair][:, u, cols])
+                    nc.sync.dma_start(out=rows[:, u, cols], in_=result[half, pair][:, u, cols])
             if tile < 7:
-                nc.sync.dma_start(out=rows[:, e, :], in_=result[half, pair][:, u, :])
+                nc.sync.dma_start(out=rows[:, u, :], in_=result[half, pair][:, u, :])
 
         interleave_g(0, 0, 84)
         quantize_g(0, 0)

@@ -19,7 +19,6 @@ PACK = 4
 SPAN = P * PACK
 BANKS = 8
 DECAY = 0.9
-G_VECTOR_SHARE = 80
 
 
 def tile_mix_kfac_ema_kernel(tc, g, am_words, am_scales, bm_words, bm_scales, mom, out):
@@ -78,7 +77,6 @@ def tile_mix_kfac_ema_kernel(tc, g, am_words, am_scales, bm_words, bm_scales, mo
 
         g_codes = {}
         g_plane = {}
-
         g_grouped = {}
 
         def interleave_g(b, a, vector_share):
@@ -91,19 +89,19 @@ def tile_mix_kfac_ema_kernel(tc, g, am_words, am_scales, bm_words, bm_scales, mo
             if vector_share < P:
                 nc.scalar.copy(out=dst[:, vector_share:], in_=src[:, vector_share:])
 
-        def quantize_g(b, a):
-            grouped = g_grouped[b, a]
-            for pair in range(2):
-                codes = sbuf("g_codes%d%d%d" % (b, a, pair), [P, 2 * P], U32)
-                plane = sbuf("g_plane%d%d%d" % (b, a, pair), [P, 2 * P], U8)
+        def quantize_g(b, a, calls):
+            slots = PACK // calls
+            for first in range(0, PACK, slots):
+                codes = sbuf("g_codes%d%d%d" % (b, a, first), [P, slots * P], U32)
+                plane = sbuf("g_plane%d%d%d" % (b, a, first), [P, slots * P], U8)
                 nc.vector.quantize_mx(
                     out=codes[:].bitcast(E5M2X4),
                     scales=plane[:],
-                    in_=grouped[:, pair * 2 * SPAN : (pair + 1) * 2 * SPAN],
+                    in_=g_grouped[b, a][:, first * SPAN : (first + slots) * SPAN],
                 )
-                for u in range(2):
-                    g_codes[b, a, 2 * pair + u] = codes[:, u * P : (u + 1) * P]
-                    g_plane[b, a, 2 * pair + u] = plane[:, u * P : (u + 1) * P]
+                for u in range(slots):
+                    g_codes[b, a, first + u] = codes[:, u * P : (u + 1) * P]
+                    g_plane[b, a, first + u] = plane[:, u * P : (u + 1) * P]
 
         h_acc = {}
 
@@ -123,11 +121,12 @@ def tile_mix_kfac_ema_kernel(tc, g, am_words, am_scales, bm_words, bm_scales, mo
 
         h_rows = {}
 
-        def drain_h(b, half, t, on_vector):
-            if t == 0:
+        def drain_h(b, half, t, pairs, on_vector=False):
+            if (b, half) not in h_rows:
                 h_rows[b, half] = sbuf("h_rows%d%d" % (b, half), [P, PACK, SPAN], BF16)
-            dst = h_rows[b, half][:, t, :]
-            src = h_acc[b, half, t][:]
+            cols = slice(pairs.start * 2 * P, pairs.stop * 2 * P)
+            dst = h_rows[b, half][:, t, cols]
+            src = h_acc[b, half, t][:, cols]
             if on_vector:
                 nc.vector.tensor_copy(out=dst, in_=src)
             else:
@@ -135,38 +134,44 @@ def tile_mix_kfac_ema_kernel(tc, g, am_words, am_scales, bm_words, bm_scales, mo
 
         h_grouped = {}
 
-        def interleave_h(b, half, pair, on_vector):
-            h_grouped[b, half, pair] = sbuf("h_grouped%d%d%d" % (b, half, pair), [P, 2 * SPAN], BF16)
-            dst = h_grouped[b, half, pair][:].rearrange("p (u c i t) -> p c t i u", u=2, i=2, t=PACK)
+        def interleave_h(b, half, pair, on_vector, groups=slice(0, P // 2)):
+            if (half, pair) not in h_grouped:
+                h_grouped[half, pair] = sbuf("h_grouped%d%d" % (half, pair), [P, PACK * SPAN], BF16)
+            part = h_grouped[half, pair][:, b * 2 * SPAN : (b + 1) * 2 * SPAN]
+            dst = part.rearrange("p (u c i t) -> p c t i u", u=2, i=2, t=PACK)
             src = h_rows[b, half][:, :, pair * 2 * P : (pair + 1) * 2 * P].rearrange("p t (c i u) -> p c t i u", i=2, u=2)
             if on_vector:
-                nc.vector.tensor_copy(out=dst, in_=src)
+                nc.vector.tensor_copy(out=dst[:, groups], in_=src[:, groups])
             else:
-                nc.scalar.copy(out=dst, in_=src)
+                nc.scalar.copy(out=dst[:, groups], in_=src[:, groups])
 
         h_codes = {}
         h_plane = {}
 
-        def quantize_h(b, half, pair):
-            h_codes[b, half, pair] = sbuf("h_codes%d%d%d" % (b, half, pair), [P, 2 * P], U32)
-            h_plane[b, half, pair] = sbuf("h_plane%d%d%d" % (b, half, pair), [P, 2 * P], U8)
+        def quantize_h(blocks, half, pair):
+            width = len(blocks) * 2 * P
+            codes = sbuf("h_codes%d%d%d" % (blocks.start, half, pair), [P, width], U32)
+            plane = sbuf("h_plane%d%d%d" % (blocks.start, half, pair), [P, width], U8)
             nc.vector.quantize_mx(
-                out=h_codes[b, half, pair][:].bitcast(E4M3X4),
-                scales=h_plane[b, half, pair][:],
-                in_=h_grouped[b, half, pair][:],
+                out=codes[:].bitcast(E4M3X4),
+                scales=plane[:],
+                in_=h_grouped[half, pair][:, blocks.start * 2 * SPAN : blocks.stop * 2 * SPAN],
             )
+            for b in blocks:
+                for u in range(2):
+                    e = 2 * (b - blocks.start) + u
+                    h_codes[b, PACK * half + 2 * pair + u] = codes[:, e * P : (e + 1) * P]
+                    h_plane[b, PACK * half + 2 * pair + u] = plane[:, e * P : (e + 1) * P]
 
         y_acc = {}
 
         def multiply_y(tile, side, b):
-            half, e = divmod(tile, PACK)
-            pair, u = divmod(e, 2)
             if b == 0:
                 y_acc[tile, side] = bank((2 * tile + side) % BANKS)
             nc.tensor.matmul_mx(
                 out=y_acc[tile, side][:],
-                lhsT=h_codes[b, half, pair][:, u * P : (u + 1) * P].bitcast(E4M3X4),
-                lhsT_scale=h_plane[b, half, pair][:, u * P : (u + 1) * P],
+                lhsT=h_codes[b, tile].bitcast(E4M3X4),
+                lhsT_scale=h_plane[b, tile],
                 rhs=bm_codes[:, b, side * 2 * SPAN : (side + 1) * 2 * SPAN].bitcast(E2M1X4),
                 rhs_scale=bm_plane[:, b, side * SPAN : (side + 1) * SPAN],
                 start=(b == 0),
@@ -180,86 +185,108 @@ def tile_mix_kfac_ema_kernel(tc, g, am_words, am_scales, bm_words, bm_scales, mo
 
         result = {}
 
-        def finish(tile):
+        def rows_of(tile):
             half, e = divmod(tile, PACK)
             pair, u = divmod(e, 2)
-            if u == 0:
-                result[half, pair] = sbuf("result%d%d" % (half, pair), [P, 2, N], F32)
             first = half * SPAN + pair * 2 * P
-            rows = out[first : first + 2 * P, :].rearrange("(q u) n -> q u n", u=2)
-            for side in range(2):
-                cols = slice(side * SPAN, (side + 1) * SPAN)
-                nc.vector.scalar_tensor_tensor(
-                    out=result[half, pair][:, u, cols],
-                    in0=mom_sb[half, pair][:, u, cols],
-                    scalar=DECAY,
-                    in1=y_acc[tile, side][:],
-                    op0=mybir.AluOpType.mult,
-                    op1=mybir.AluOpType.add,
-                )
-                if tile == 7:
-                    nc.sync.dma_start(out=rows[:, u, cols], in_=result[half, pair][:, u, cols])
-            if tile < 7:
-                nc.sync.dma_start(out=rows[:, u, :], in_=result[half, pair][:, u, :])
+            return out[first : first + 2 * P, :].rearrange("(q u) n -> q u n", u=2)[:, u, :]
+
+        def mom_of(tile):
+            half, e = divmod(tile, PACK)
+            pair, u = divmod(e, 2)
+            return mom_sb[half, pair][:, u, :]
+
+        def result_of(tile):
+            if tile not in result:
+                result[tile] = sbuf("result%d" % tile, [P, N], F32)
+            return result[tile]
+
+        def finish_bank(tile, side):
+            cols = slice(side * SPAN, (side + 1) * SPAN)
+            nc.vector.scalar_tensor_tensor(
+                out=result_of(tile)[:, cols],
+                in0=mom_of(tile)[:, cols],
+                scalar=DECAY,
+                in1=y_acc[tile, side][:],
+                op0=mybir.AluOpType.mult,
+                op1=mybir.AluOpType.add,
+            )
+
+        def store(tile, cols=slice(0, N)):
+            nc.sync.dma_start(out=rows_of(tile)[:, cols], in_=result[tile][:, cols])
+
+        def finish(tile):
+            finish_bank(tile, 0)
+            finish_bank(tile, 1)
+            store(tile)
+
+        both = range(2)
+        low = range(0, 1)
+        high = range(1, 2)
 
         interleave_g(0, 0, 84)
-        quantize_g(0, 0)
+        quantize_g(0, 0, 2)
         multiply_h(0, 0, 0)
         multiply_h(0, 0, 1, range(2))
         interleave_g(0, 1, 84)
-        quantize_g(0, 1)
+        quantize_g(0, 1, 2)
         multiply_h(0, 1, 0)
         multiply_h(0, 0, 1, range(2, 4))
         multiply_h(0, 1, 1)
         for t in range(PACK):
-            drain_h(0, 0, t, t == 1)
-        for t in range(PACK):
-            drain_h(0, 1, t, False)
+            drain_h(0, 0, t, both)
         interleave_g(1, 0, P)
-        interleave_h(0, 0, 0, True)
-        quantize_g(1, 0)
+        drain_h(0, 1, 0, low, True)
+        quantize_g(1, 0, 1)
+        drain_h(0, 1, 0, high)
         multiply_h(1, 0, 0)
-        multiply_h(1, 0, 1, range(2))
-        interleave_g(1, 1, 96)
-        quantize_h(0, 0, 0)
-        quantize_g(1, 1)
+        interleave_g(1, 1, 84)
+        interleave_h(0, 0, 0, True, slice(0, 32))
+        quantize_g(1, 1, 2)
+        for t in range(1, 4):
+            drain_h(0, 1, t, both)
+        multiply_h(1, 0, 1, range(1))
         multiply_h(1, 1, 0)
-        multiply_h(1, 0, 1, range(2, 4))
-        interleave_h(0, 1, 0, False)
-        interleave_h(0, 0, 1, True)
-        for t in range(PACK):
-            drain_h(1, 0, t, t % 2 == 1)
-        quantize_h(0, 0, 1)
+        multiply_h(1, 0, 1, range(1, 4))
         multiply_h(1, 1, 1)
-        for tile in range(2):
-            for side in range(2):
-                multiply_y(tile, side, 0)
-        interleave_h(1, 0, 0, True)
-        interleave_h(1, 0, 1, False)
-        quantize_h(0, 1, 0)
-        quantize_h(1, 0, 0)
-        for tile in range(2):
-            for side in range(2):
-                multiply_y(tile, side, 1)
+        interleave_h(0, 0, 0, True, slice(32, 64))
+        interleave_h(0, 0, 1, True)
+        quantize_h(low, 0, 0)
         for t in range(PACK):
-            drain_h(1, 1, t, False)
-        quantize_h(1, 0, 1)
+            drain_h(1, 0, t, low, t == 3)
+        quantize_h(low, 0, 1)
+        for t in range(PACK):
+            drain_h(1, 0, t, high)
+        interleave_h(1, 0, 0, True)
+        interleave_h(0, 1, 0, True, slice(0, 32))
+        quantize_h(high, 0, 0)
+        multiply_tile(0)
+        multiply_tile(1)
+        interleave_h(0, 1, 0, True, slice(32, 64))
+        drain_h(1, 1, 0, both)
+        interleave_h(1, 0, 1, False)
+        for t in range(1, PACK):
+            drain_h(1, 1, t, both)
+        quantize_h(low, 1, 0)
+        interleave_h(1, 1, 0, False)
+        interleave_h(0, 1, 1, False)
+        interleave_h(1, 1, 1, False)
+        finish(0)
+        quantize_h(high, 0, 1)
         multiply_tile(2)
         multiply_tile(3)
-        interleave_h(1, 1, 0, False)
-        for b in range(2):
-            interleave_h(b, 1, 1, False)
-        finish(0)
         finish(1)
         finish(2)
-        quantize_h(1, 1, 0)
+        quantize_h(high, 1, 0)
         multiply_tile(4)
         multiply_tile(5)
         finish(3)
         finish(4)
-        for b in range(2):
-            quantize_h(b, 1, 1)
+        quantize_h(both, 1, 1)
         multiply_tile(6)
         multiply_tile(7)
-        for tile in range(5, 8):
-            finish(tile)
+        finish(5)
+        finish(6)
+        for side in range(2):
+            finish_bank(7, side)
+            store(7, slice(side * SPAN, (side + 1) * SPAN))

@@ -46,10 +46,16 @@ def tile_mix_kfac_ema_kernel(tc, g, am_words, am_scales, bm_words, bm_scales, mo
 
         g_raw = {}
 
-        def load_g(b, a):
-            g_raw[b, a] = sbuf("g_raw%d%d" % (b, a), [P, PACK, SPAN], F32)
-            rows = g[a * SPAN : (a + 1) * SPAN, b * SPAN : (b + 1) * SPAN]
-            nc.sync.dma_start(out=g_raw[b, a][:], in_=rows.rearrange("(p j) l -> p j l", j=PACK))
+        def load_g(b, a, pieces=1):
+            width = SPAN // pieces
+            for piece in range(pieces):
+                load_g_piece(b, a, piece, width)
+
+        def load_g_piece(b, a, piece, width):
+            g_raw[b, a, piece] = sbuf("g_raw%d%d%d" % (b, a, piece), [P, PACK, width], F32)
+            first = b * SPAN + piece * width
+            rows = g[a * SPAN : (a + 1) * SPAN, first : first + width]
+            nc.sync.dma_start(out=g_raw[b, a, piece][:], in_=rows.rearrange("(p j) l -> p j l", j=PACK))
 
         am_codes = {}
 
@@ -79,14 +85,15 @@ def tile_mix_kfac_ema_kernel(tc, g, am_words, am_scales, bm_words, bm_scales, mo
         g_plane = {}
         g_grouped = {}
 
-        def interleave_g(b, a, vector_share):
-            grouped = sbuf("g_grouped%d%d" % (b, a), [P, PACK * SPAN], BF16)
-            g_grouped[b, a] = grouped
-            dst = grouped[:].rearrange("p (t q j) -> p q j t", t=PACK, j=PACK)
-            src = g_raw[b, a][:].rearrange("p j (q t) -> p q j t", t=PACK)
+        def interleave_g(b, a, vector_share, piece=0):
+            if piece == 0:
+                g_grouped[b, a] = sbuf("g_grouped%d%d" % (b, a), [P, PACK * SPAN], BF16)
+            src = g_raw[b, a, piece][:].rearrange("p j (q t) -> p q j t", t=PACK)
+            count = src.shape[1]
+            dst = g_grouped[b, a][:].rearrange("p (t q j) -> p q j t", t=PACK, j=PACK)[:, piece * count : (piece + 1) * count]
             if vector_share > 0:
                 nc.vector.tensor_copy(out=dst[:, :vector_share], in_=src[:, :vector_share])
-            if vector_share < P:
+            if vector_share < count:
                 nc.scalar.copy(out=dst[:, vector_share:], in_=src[:, vector_share:])
 
         def quantize_g(b, a, calls):
@@ -220,6 +227,11 @@ def tile_mix_kfac_ema_kernel(tc, g, am_words, am_scales, bm_words, bm_scales, mo
             finish_bank(tile, 1)
             store(tile)
 
+        def finish_by_bank(tile):
+            for side in range(2):
+                finish_bank(tile, side)
+                store(tile, slice(side * SPAN, (side + 1) * SPAN))
+
         both = range(2)
         low = range(0, 1)
         high = range(1, 2)
@@ -285,8 +297,6 @@ def tile_mix_kfac_ema_kernel(tc, g, am_words, am_scales, bm_words, bm_scales, mo
         quantize_h(both, 1, 1)
         multiply_tile(6)
         multiply_tile(7)
-        finish(5)
-        finish(6)
-        for side in range(2):
-            finish_bank(7, side)
-            store(7, slice(side * SPAN, (side + 1) * SPAN))
+        finish_by_bank(5)
+        finish_by_bank(6)
+        finish_by_bank(7)

@@ -19,6 +19,7 @@ PACK = 4
 SPAN = P * PACK
 BANKS = 8
 DECAY = 0.9
+Y_BANK_PAIRS = 3
 
 
 def tile_mix_kfac_ema_kernel(tc, g, am_words, am_scales, bm_words, bm_scales, mom, out):
@@ -74,12 +75,16 @@ def tile_mix_kfac_ema_kernel(tc, g, am_words, am_scales, bm_words, bm_scales, mo
         nc.sync.dma_start(out=bm_codes[:].bitcast(I32), in_=bm_words.rearrange("a p c -> p a c").bitcast(I32))
         load_plane(bm_plane, bm_scales)
         mom_sb = {}
-        for half in range(2):
-            for pair in range(2):
-                first = half * SPAN + pair * 2 * P
-                rows = mom[first : first + 2 * P, :].rearrange("(q u) n -> q u n", u=2)
-                mom_sb[half, pair] = sbuf("mom%d%d" % (half, pair), [P, 2, N], F32)
-                nc.sync.dma_start(out=mom_sb[half, pair][:], in_=rows)
+
+        def load_mom(pairs):
+            rows = mom[pairs.start * 2 * P : pairs.stop * 2 * P, :].rearrange("(r q u) n -> q r (u n)", q=P, u=2)
+            held = sbuf("mom%d" % pairs.start, [P, len(pairs), 2 * N], F32)
+            nc.sync.dma_start(out=held[:], in_=rows)
+            for pair in pairs:
+                mom_sb[pair] = held[:, pair - pairs.start, :]
+
+        for pair in range(PACK):
+            load_mom(range(pair, pair + 1))
 
         g_codes = {}
         g_plane = {}
@@ -141,11 +146,14 @@ def tile_mix_kfac_ema_kernel(tc, g, am_words, am_scales, bm_words, bm_scales, mo
 
         h_grouped = {}
 
+        def grouped_part(b, half, pair, shared=False):
+            if (b, half, pair) not in h_grouped:
+                tag = "shared" if shared else "h_grouped%d%d%d" % (b, half, pair)
+                h_grouped[b, half, pair] = sb.tile([P, 2 * SPAN], BF16, name="h_grouped", tag=tag, align_bytes=64)
+            return h_grouped[b, half, pair][:]
+
         def interleave_h(b, half, pair, on_vector, groups=slice(0, P // 2)):
-            if (half, pair) not in h_grouped:
-                h_grouped[half, pair] = sbuf("h_grouped%d%d" % (half, pair), [P, PACK * SPAN], BF16)
-            part = h_grouped[half, pair][:, b * 2 * SPAN : (b + 1) * 2 * SPAN]
-            dst = part.rearrange("p (u c i t) -> p c t i u", u=2, i=2, t=PACK)
+            dst = grouped_part(b, half, pair).rearrange("p (u c i t) -> p c t i u", u=2, i=2, t=PACK)
             src = h_rows[b, half][:, :, pair * 2 * P : (pair + 1) * 2 * P].rearrange("p t (c i u) -> p c t i u", i=2, u=2)
             if on_vector:
                 nc.vector.tensor_copy(out=dst[:, groups], in_=src[:, groups])
@@ -155,26 +163,47 @@ def tile_mix_kfac_ema_kernel(tc, g, am_words, am_scales, bm_words, bm_scales, mo
         h_codes = {}
         h_plane = {}
 
-        def quantize_h(blocks, half, pair):
-            width = len(blocks) * 2 * P
-            codes = sbuf("h_codes%d%d%d" % (blocks.start, half, pair), [P, width], U32)
-            plane = sbuf("h_plane%d%d%d" % (blocks.start, half, pair), [P, width], U8)
-            nc.vector.quantize_mx(
-                out=codes[:].bitcast(E4M3X4),
-                scales=plane[:],
-                in_=h_grouped[half, pair][:, blocks.start * 2 * SPAN : blocks.stop * 2 * SPAN],
+        def quantize_h(b, half, pair):
+            codes = sbuf("h_codes%d%d%d" % (b, half, pair), [P, 2 * P], U32)
+            plane = sbuf("h_plane%d%d%d" % (b, half, pair), [P, 2 * P], U8)
+            nc.vector.quantize_mx(out=codes[:].bitcast(E4M3X4), scales=plane[:], in_=grouped_part(b, half, pair))
+            for u in range(2):
+                h_codes[b, PACK * half + 2 * pair + u] = codes[:, u * P : (u + 1) * P]
+                h_plane[b, PACK * half + 2 * pair + u] = plane[:, u * P : (u + 1) * P]
+
+        tile_rows = {}
+        tile_grouped = {}
+
+        def drain_tile(u, t, on_vector):
+            if u not in tile_rows:
+                tile_rows[u] = sbuf("tile_rows%d" % u, [P, PACK, P], BF16)
+            src = h_acc[1, 0, t][:, : 2 * P].rearrange("p (q u) -> p u q", u=2)[:, u, :]
+            if on_vector:
+                nc.vector.tensor_copy(out=tile_rows[u][:, t, :], in_=src)
+            else:
+                nc.scalar.copy(out=tile_rows[u][:, t, :], in_=src)
+
+        def interleave_tile(u):
+            part = grouped_part(1, 0, 0)[:, u * SPAN : (u + 1) * SPAN]
+            nc.vector.tensor_copy(
+                out=part.rearrange("p (c i t) -> p c t i", i=4, t=PACK),
+                in_=tile_rows[u][:].rearrange("p t (c i) -> p c t i", i=4),
             )
-            for b in blocks:
-                for u in range(2):
-                    e = 2 * (b - blocks.start) + u
-                    h_codes[b, PACK * half + 2 * pair + u] = codes[:, e * P : (e + 1) * P]
-                    h_plane[b, PACK * half + 2 * pair + u] = plane[:, e * P : (e + 1) * P]
+
+        def quantize_tile(u):
+            codes = sbuf("tile_codes%d" % u, [P, P], U32)
+            plane = sbuf("tile_plane%d" % u, [P, P], U8)
+            nc.vector.quantize_mx(
+                out=codes[:].bitcast(E4M3X4), scales=plane[:], in_=grouped_part(1, 0, 0)[:, u * SPAN : (u + 1) * SPAN]
+            )
+            h_codes[1, u] = codes[:]
+            h_plane[1, u] = plane[:]
 
         y_acc = {}
 
         def multiply_y(tile, side, b):
             if b == 0:
-                y_acc[tile, side] = bank((2 * tile + side) % BANKS)
+                y_acc[tile, side] = bank(2 * (tile % Y_BANK_PAIRS) + side)
             nc.tensor.matmul_mx(
                 out=y_acc[tile, side][:],
                 lhsT=h_codes[b, tile].bitcast(E4M3X4),
@@ -192,45 +221,35 @@ def tile_mix_kfac_ema_kernel(tc, g, am_words, am_scales, bm_words, bm_scales, mo
 
         result = {}
 
-        def rows_of(tile):
-            half, e = divmod(tile, PACK)
-            pair, u = divmod(e, 2)
-            first = half * SPAN + pair * 2 * P
-            return out[first : first + 2 * P, :].rearrange("(q u) n -> q u n", u=2)[:, u, :]
-
-        def mom_of(tile):
-            half, e = divmod(tile, PACK)
-            pair, u = divmod(e, 2)
-            return mom_sb[half, pair][:, u, :]
-
-        def result_of(tile):
-            if tile not in result:
-                result[tile] = sbuf("result%d" % tile, [P, N], F32)
-            return result[tile]
-
         def finish_bank(tile, side):
-            cols = slice(side * SPAN, (side + 1) * SPAN)
+            pair, u = divmod(tile, 2)
+            if pair not in result:
+                result[pair] = sbuf("result%d" % pair, [P, 2 * N], F32)
+            cols = slice(u * N + side * SPAN, u * N + (side + 1) * SPAN)
             nc.vector.scalar_tensor_tensor(
-                out=result_of(tile)[:, cols],
-                in0=mom_of(tile)[:, cols],
+                out=result[pair][:, cols],
+                in0=mom_sb[pair][:, cols],
                 scalar=DECAY,
                 in1=y_acc[tile, side][:],
                 op0=mybir.AluOpType.mult,
                 op1=mybir.AluOpType.add,
             )
 
-        def store(tile, cols=slice(0, N)):
-            nc.sync.dma_start(out=rows_of(tile)[:, cols], in_=result[tile][:, cols])
+        def store(pair, cols):
+            rows = out[pair * 2 * P : (pair + 1) * 2 * P, :].rearrange("(q u) n -> q (u n)", u=2)
+            nc.sync.dma_start(out=rows[:, cols], in_=result[pair][:, cols])
 
         def finish(tile):
             finish_bank(tile, 0)
             finish_bank(tile, 1)
-            store(tile)
 
-        def finish_by_bank(tile):
-            for side in range(2):
-                finish_bank(tile, side)
-                store(tile, slice(side * SPAN, (side + 1) * SPAN))
+        def store_tile(tile):
+            pair, u = divmod(tile, 2)
+            store(pair, slice(u * N, (u + 1) * N))
+
+        def store_bank(tile, side):
+            pair, u = divmod(tile, 2)
+            store(pair, slice(u * N + side * SPAN, u * N + (side + 1) * SPAN))
 
         both = range(2)
         low = range(0, 1)
@@ -239,11 +258,11 @@ def tile_mix_kfac_ema_kernel(tc, g, am_words, am_scales, bm_words, bm_scales, mo
         interleave_g(0, 0, 84)
         quantize_g(0, 0, 2)
         multiply_h(0, 0, 0)
-        multiply_h(0, 0, 1, range(2))
+        multiply_h(0, 0, 1, range(3))
         interleave_g(0, 1, 84)
         quantize_g(0, 1, 2)
         multiply_h(0, 1, 0)
-        multiply_h(0, 0, 1, range(2, 4))
+        multiply_h(0, 0, 1, range(3, 4))
         multiply_h(0, 1, 1)
         for t in range(PACK):
             drain_h(0, 0, t, both)
@@ -253,7 +272,7 @@ def tile_mix_kfac_ema_kernel(tc, g, am_words, am_scales, bm_words, bm_scales, mo
         drain_h(0, 1, 0, high)
         multiply_h(1, 0, 0)
         interleave_g(1, 1, 84)
-        interleave_h(0, 0, 0, True, slice(0, 32))
+        interleave_h(0, 0, 0, True, slice(0, 20))
         quantize_g(1, 1, 2)
         for t in range(1, 4):
             drain_h(0, 1, t, both)
@@ -261,42 +280,61 @@ def tile_mix_kfac_ema_kernel(tc, g, am_words, am_scales, bm_words, bm_scales, mo
         multiply_h(1, 1, 0)
         multiply_h(1, 0, 1, range(1, 4))
         multiply_h(1, 1, 1)
-        interleave_h(0, 0, 0, True, slice(32, 64))
+        interleave_h(0, 0, 0, True, slice(20, 64))
         interleave_h(0, 0, 1, True)
-        quantize_h(low, 0, 0)
+        quantize_h(0, 0, 0)
         for t in range(PACK):
-            drain_h(1, 0, t, low, t == 3)
-        quantize_h(low, 0, 1)
+            drain_tile(0, t, t == 3)
         for t in range(PACK):
-            drain_h(1, 0, t, high)
-        interleave_h(1, 0, 0, True)
-        interleave_h(0, 1, 0, True, slice(0, 32))
-        quantize_h(high, 0, 0)
+            drain_tile(1, t, t == 3)
+        drain_h(1, 0, 0, high)
+        drain_h(1, 0, 1, high)
+        interleave_tile(0)
+        interleave_tile(1)
+        quantize_tile(0)
+        quantize_tile(1)
+        drain_h(1, 0, 2, high)
+        drain_h(1, 0, 3, high)
+        quantize_h(0, 0, 1)
         multiply_tile(0)
         multiply_tile(1)
-        interleave_h(0, 1, 0, True, slice(32, 64))
-        drain_h(1, 1, 0, both)
+        drain_h(1, 1, 0, low)
         interleave_h(1, 0, 1, False)
-        for t in range(1, PACK):
-            drain_h(1, 1, t, both)
-        quantize_h(low, 1, 0)
-        interleave_h(1, 1, 0, False)
-        interleave_h(0, 1, 1, False)
-        interleave_h(1, 1, 1, False)
+        interleave_h(0, 1, 0, True)
+        drain_h(1, 1, 0, high)
+        drain_h(1, 1, 1, both)
+        drain_h(1, 1, 2, low)
+        drain_h(1, 1, 3, low)
+        drain_h(1, 1, 2, high)
         finish(0)
-        quantize_h(high, 0, 1)
+        store_tile(0)
+        quantize_h(1, 0, 1)
+        quantize_h(0, 1, 0)
         multiply_tile(2)
         multiply_tile(3)
+        interleave_h(1, 1, 0, False)
+        drain_h(1, 1, 3, high)
+        interleave_h(0, 1, 1, False)
+        interleave_h(1, 1, 1, False)
         finish(1)
+        store_tile(1)
         finish(2)
-        quantize_h(high, 1, 0)
+        store_tile(2)
+        quantize_h(1, 1, 0)
+
         multiply_tile(4)
         multiply_tile(5)
         finish(3)
-        finish(4)
-        quantize_h(both, 1, 1)
+        store_tile(3)
+        finish_bank(4, 0)
+        store_bank(4, 0)
+        quantize_h(0, 1, 1)
+        finish_bank(4, 1)
+        store_bank(4, 1)
+        quantize_h(1, 1, 1)
         multiply_tile(6)
         multiply_tile(7)
-        finish_by_bank(5)
-        finish_by_bank(6)
-        finish_by_bank(7)
+        for tile in range(5, 8):
+            for side in range(2):
+                finish_bank(tile, side)
+                store_bank(tile, side)

@@ -90,16 +90,14 @@ def tile_mix_kfac_ema_kernel(tc, g, am_words, am_scales, bm_words, bm_scales, mo
         g_plane = {}
         g_grouped = {}
 
-        def interleave_g(b, a, vector_share, piece=0):
-            if piece == 0:
-                g_grouped[b, a] = sbuf("g_grouped%d%d" % (b, a), [P, PACK * SPAN], BF16)
-            src = g_raw[b, a, piece][:].rearrange("p j (q t) -> p q j t", t=PACK)
-            count = src.shape[1]
-            dst = g_grouped[b, a][:].rearrange("p (t q j) -> p q j t", t=PACK, j=PACK)[:, piece * count : (piece + 1) * count]
-            if vector_share > 0:
-                nc.vector.tensor_copy(out=dst[:, :vector_share], in_=src[:, :vector_share])
-            if vector_share < count:
-                nc.scalar.copy(out=dst[:, vector_share:], in_=src[:, vector_share:])
+        def interleave_g(b, a, vector_share):
+            g_grouped[b, a] = sbuf("g_grouped%d%d" % (b, a), [P, PACK * SPAN], BF16)
+            src = g_raw[b, a, 0][:].rearrange("p j (c e h t) -> p h c j e t", e=2, h=2, t=2)
+            dst = g_grouped[b, a][:].rearrange("p (h t c e j) -> p h c j e t", h=2, t=2, e=2, j=PACK)
+            nc.vector.tensor_copy(out=dst[:, 0], in_=src[:, 0])
+            nc.vector.tensor_copy(out=dst[:, 1, :vector_share], in_=src[:, 1, :vector_share])
+            if vector_share < P // 2:
+                nc.scalar.copy(out=dst[:, 1, vector_share:], in_=src[:, 1, vector_share:])
 
         def quantize_g(b, a, calls):
             slots = PACK // calls
@@ -255,24 +253,23 @@ def tile_mix_kfac_ema_kernel(tc, g, am_words, am_scales, bm_words, bm_scales, mo
         low = range(0, 1)
         high = range(1, 2)
 
-        interleave_g(0, 0, 84)
+        interleave_g(0, 0, 20)
         quantize_g(0, 0, 2)
         multiply_h(0, 0, 0)
         multiply_h(0, 0, 1, range(3))
-        interleave_g(0, 1, 84)
+        interleave_g(0, 1, 20)
         quantize_g(0, 1, 2)
         multiply_h(0, 1, 0)
         multiply_h(0, 0, 1, range(3, 4))
         multiply_h(0, 1, 1)
         for t in range(PACK):
             drain_h(0, 0, t, both)
-        interleave_g(1, 0, P)
-        drain_h(0, 1, 0, low, True)
-        quantize_g(1, 0, 1)
-        drain_h(0, 1, 0, high)
+        interleave_g(1, 0, P // 2)
+        quantize_g(1, 0, 2)
+        drain_h(0, 1, 0, both)
         multiply_h(1, 0, 0)
-        interleave_g(1, 1, 84)
-        interleave_h(0, 0, 0, True, slice(0, 20))
+        interleave_h(0, 0, 0, True, slice(0, 16))
+        interleave_g(1, 1, 20)
         quantize_g(1, 1, 2)
         for t in range(1, 4):
             drain_h(0, 1, t, both)
@@ -280,7 +277,7 @@ def tile_mix_kfac_ema_kernel(tc, g, am_words, am_scales, bm_words, bm_scales, mo
         multiply_h(1, 1, 0)
         multiply_h(1, 0, 1, range(1, 4))
         multiply_h(1, 1, 1)
-        interleave_h(0, 0, 0, True, slice(20, 64))
+        interleave_h(0, 0, 0, True, slice(16, 64))
         interleave_h(0, 0, 1, True)
         quantize_h(0, 0, 0)
         for t in range(PACK):

@@ -30,7 +30,7 @@ def tile_mix_kfac_ema_kernel(tc, g, am_words, am_scales, bm_words, bm_scales, mo
         ctx.enter_context(tc.manual_schedule())
 
         def sbuf(name, shape, dtype):
-            return sb.tile(shape, dtype, name=name, align_bytes=64)
+            return sb.tile(shape, dtype, name=name, align_bytes=256)
 
         def bank(index):
             return psum.tile([P, SPAN], F32, name="acc", tag="bank%d" % index)
@@ -147,7 +147,7 @@ def tile_mix_kfac_ema_kernel(tc, g, am_words, am_scales, bm_words, bm_scales, mo
         def grouped_part(b, half, pair, shared=False):
             if (b, half, pair) not in h_grouped:
                 tag = "shared" if shared else "h_grouped%d%d%d" % (b, half, pair)
-                h_grouped[b, half, pair] = sb.tile([P, 2 * SPAN], BF16, name="h_grouped", tag=tag, align_bytes=64)
+                h_grouped[b, half, pair] = sb.tile([P, 2 * SPAN], BF16, name="h_grouped", tag=tag, align_bytes=256)
             return h_grouped[b, half, pair][:]
 
         def interleave_h(b, half, pair, on_vector, groups=slice(0, P // 2)):

@@ -19,7 +19,7 @@ PACK = 4
 SPAN = P * PACK
 BANKS = 8
 DECAY = 0.9
-Y_BANK_PAIRS = 3
+ROWS = 4
 
 
 def tile_mix_kfac_ema_kernel(tc, g, am_words, am_scales, bm_words, bm_scales, mom, out):
@@ -47,22 +47,142 @@ def tile_mix_kfac_ema_kernel(tc, g, am_words, am_scales, bm_words, bm_scales, mo
 
         g_raw = {}
 
-        def load_g(b, a, pieces=1):
-            width = SPAN // pieces
-            for piece in range(pieces):
-                load_g_piece(b, a, piece, width)
-
-        def load_g_piece(b, a, piece, width):
-            g_raw[b, a, piece] = sbuf("g_raw%d%d%d" % (b, a, piece), [P, PACK, width], F32)
-            first = b * SPAN + piece * width
-            rows = g[a * SPAN : (a + 1) * SPAN, first : first + width]
-            nc.sync.dma_start(out=g_raw[b, a, piece][:], in_=rows.rearrange("(p j) l -> p j l", j=PACK))
+        def load_g(b, a):
+            held = sbuf("g_raw%d%d" % (b, a), [P, PACK, SPAN], F32)
+            rows = g[a * SPAN : (a + 1) * SPAN, b * SPAN : (b + 1) * SPAN]
+            nc.sync.dma_start(out=held[:], in_=rows.rearrange("(p j) l -> p j l", j=PACK))
+            g_raw[b, a] = held[:]
 
         am_codes = {}
 
         def load_am(a):
             am_codes[a] = sbuf("am_codes%d" % a, [P, 2 * M], U8)
             nc.sync.dma_start(out=am_codes[a][:].bitcast(I32), in_=am_words[a].bitcast(I32))
+
+        def half_rows(matrix, half):
+            return matrix[half * SPAN : (half + 1) * SPAN, :].rearrange("(q w) n -> q (w n)", w=ROWS)
+
+        mom_sb = {}
+
+        def load_mom(tiles):
+            half, first = divmod(tiles.start, ROWS)
+            held = sbuf("mom%d" % tiles.start, [P, len(tiles) * N], F32)
+            nc.sync.dma_start(out=held[:], in_=half_rows(mom, half)[:, first * N : (first + len(tiles)) * N])
+            for tile in tiles:
+                mom_sb[tile] = held[:, (tile - tiles.start) * N : (tile - tiles.start + 1) * N]
+
+        g_codes = {}
+        g_plane = {}
+        g_grouped = {}
+
+        def interleave_g(b, a, vector_share):
+            g_grouped[b, a] = sbuf("g_grouped%d%d" % (b, a), [P, PACK * SPAN], BF16)
+            src = g_raw[b, a].rearrange("p j (c e h t) -> p h c j e t", e=2, h=2, t=2)
+            dst = g_grouped[b, a][:].rearrange("p (h t c e j) -> p h c j e t", h=2, t=2, e=2, j=PACK)
+            nc.vector.tensor_copy(out=dst[:, 0], in_=src[:, 0])
+            nc.vector.tensor_copy(out=dst[:, 1, :vector_share], in_=src[:, 1, :vector_share])
+            if vector_share < P // 2:
+                nc.scalar.copy(out=dst[:, 1, vector_share:], in_=src[:, 1, vector_share:])
+
+        def quantize_g(b, a):
+            for first in range(0, PACK, 2):
+                codes = sbuf("g_codes%d%d%d" % (b, a, first), [P, 2 * P], U32)
+                plane = sbuf("g_plane%d%d%d" % (b, a, first), [P, 2 * P], U8)
+                nc.vector.quantize_mx(
+                    out=codes[:].bitcast(E5M2X4),
+                    scales=plane[:],
+                    in_=g_grouped[b, a][:, first * SPAN : (first + 2) * SPAN],
+                )
+                for u in range(2):
+                    g_codes[b, a, first + u] = codes[:, u * P : (u + 1) * P]
+                    g_plane[b, a, first + u] = plane[:, u * P : (u + 1) * P]
+
+        h_acc = {}
+
+        def pass_h(b, a, strip, t):
+            if a == 0 and t == 0:
+                h_acc[b, strip] = bank(strip)
+            nc.tensor.matmul_mx(
+                out=h_acc[b, strip][:, t * P : (t + 1) * P],
+                lhsT=g_codes[b, a, t].bitcast(E5M2X4),
+                lhsT_scale=g_plane[b, a, t],
+                rhs=am_codes[a][:, strip * 2 * P : (strip + 1) * 2 * P].bitcast(E2M1X4),
+                rhs_scale=am_plane[:, a, strip * P : (strip + 1) * P],
+                start=(a == 0 and t == 0),
+                stop=(a == 1 and t == PACK - 1),
+            )
+
+        def multiply_h(b, a, strips):
+            for strip in strips:
+                for t in range(PACK):
+                    pass_h(b, a, strip, t)
+
+        h_grouped = {}
+
+        def drain_h(b, strip, on_vector=False):
+            half, part = divmod(strip, ROWS)
+            if (b, half) not in h_grouped:
+                h_grouped[b, half] = sbuf("h_grouped%d%d" % (b, half), [P, ROWS * SPAN], BF16)
+            width = P // ROWS
+            dst = h_grouped[b, half][:].rearrange("p (w q t) -> p w q t", w=ROWS, t=PACK)[:, :, part * width : (part + 1) * width, :]
+            src = h_acc[b, strip][:].rearrange("p (t q w) -> p w q t", t=PACK, w=ROWS)
+            if on_vector:
+                nc.vector.tensor_copy(out=dst, in_=src)
+            else:
+                nc.scalar.copy(out=dst, in_=src)
+
+        h_codes = {}
+        h_plane = {}
+
+        def quantize_h(b, tiles):
+            half, first = divmod(tiles.start, ROWS)
+            codes = sbuf("h_codes%d%d" % (b, tiles.start), [P, len(tiles) * P], U32)
+            plane = sbuf("h_plane%d%d" % (b, tiles.start), [P, len(tiles) * P], U8)
+            nc.vector.quantize_mx(
+                out=codes[:].bitcast(E4M3X4),
+                scales=plane[:],
+                in_=h_grouped[b, half][:, first * SPAN : (first + len(tiles)) * SPAN],
+            )
+            for u in range(len(tiles)):
+                h_codes[b, tiles.start + u] = codes[:, u * P : (u + 1) * P]
+                h_plane[b, tiles.start + u] = plane[:, u * P : (u + 1) * P]
+
+        y_acc = {}
+
+        def multiply_y(tile):
+            for side in range(2):
+                y_acc[tile, side] = bank((2 * tile + side) % BANKS)
+                for b in range(2):
+                    nc.tensor.matmul_mx(
+                        out=y_acc[tile, side][:],
+                        lhsT=h_codes[b, tile].bitcast(E4M3X4),
+                        lhsT_scale=h_plane[b, tile],
+                        rhs=bm_codes[:, b, side * 2 * SPAN : (side + 1) * 2 * SPAN].bitcast(E2M1X4),
+                        rhs_scale=bm_plane[:, b, side * SPAN : (side + 1) * SPAN],
+                        start=(b == 0),
+                        stop=(b == 1),
+                    )
+
+        result = {}
+
+        def finish(tile):
+            half, w = divmod(tile, ROWS)
+            if half not in result:
+                result[half] = sbuf("result%d" % half, [P, ROWS * N], F32)
+            for side in range(2):
+                nc.vector.scalar_tensor_tensor(
+                    out=result[half][:, w * N + side * SPAN : w * N + (side + 1) * SPAN],
+                    in0=mom_sb[tile][:, side * SPAN : (side + 1) * SPAN],
+                    scalar=DECAY,
+                    in1=y_acc[tile, side][:],
+                    op0=mybir.AluOpType.mult,
+                    op1=mybir.AluOpType.add,
+                )
+
+        def store(tiles):
+            half, first = divmod(tiles.start, ROWS)
+            cols = slice(first * N, (first + len(tiles)) * N)
+            nc.sync.dma_start(out=half_rows(out, half)[:, cols], in_=result[half][:, cols])
 
         load_g(0, 0)
         load_am(0)
@@ -74,264 +194,52 @@ def tile_mix_kfac_ema_kernel(tc, g, am_words, am_scales, bm_words, bm_scales, mo
         bm_codes = sbuf("bm_codes", [P, 2, 2 * N], U8)
         nc.sync.dma_start(out=bm_codes[:].bitcast(I32), in_=bm_words.rearrange("a p c -> p a c").bitcast(I32))
         load_plane(bm_plane, bm_scales)
-        mom_sb = {}
-
-        def load_mom(pairs):
-            rows = mom[pairs.start * 2 * P : pairs.stop * 2 * P, :].rearrange("(r q u) n -> q r (u n)", q=P, u=2)
-            held = sbuf("mom%d" % pairs.start, [P, len(pairs), 2 * N], F32)
-            nc.sync.dma_start(out=held[:], in_=rows)
-            for pair in pairs:
-                mom_sb[pair] = held[:, pair - pairs.start, :]
-
-        for pair in range(PACK):
-            load_mom(range(pair, pair + 1))
-
-        g_codes = {}
-        g_plane = {}
-        g_grouped = {}
-
-        def interleave_g(b, a, vector_share):
-            g_grouped[b, a] = sbuf("g_grouped%d%d" % (b, a), [P, PACK * SPAN], BF16)
-            src = g_raw[b, a, 0][:].rearrange("p j (c e h t) -> p h c j e t", e=2, h=2, t=2)
-            dst = g_grouped[b, a][:].rearrange("p (h t c e j) -> p h c j e t", h=2, t=2, e=2, j=PACK)
-            nc.vector.tensor_copy(out=dst[:, 0], in_=src[:, 0])
-            nc.vector.tensor_copy(out=dst[:, 1, :vector_share], in_=src[:, 1, :vector_share])
-            if vector_share < P // 2:
-                nc.scalar.copy(out=dst[:, 1, vector_share:], in_=src[:, 1, vector_share:])
-
-        def quantize_g(b, a, calls):
-            slots = PACK // calls
-            for first in range(0, PACK, slots):
-                codes = sbuf("g_codes%d%d%d" % (b, a, first), [P, slots * P], U32)
-                plane = sbuf("g_plane%d%d%d" % (b, a, first), [P, slots * P], U8)
-                nc.vector.quantize_mx(
-                    out=codes[:].bitcast(E5M2X4),
-                    scales=plane[:],
-                    in_=g_grouped[b, a][:, first * SPAN : (first + slots) * SPAN],
-                )
-                for u in range(slots):
-                    g_codes[b, a, first + u] = codes[:, u * P : (u + 1) * P]
-                    g_plane[b, a, first + u] = plane[:, u * P : (u + 1) * P]
-
-        h_acc = {}
-
-        def multiply_h(b, a, half, slots=range(PACK)):
-            for t in slots:
-                if a == 0:
-                    h_acc[b, half, t] = bank(PACK * half + t)
-                nc.tensor.matmul_mx(
-                    out=h_acc[b, half, t][:],
-                    lhsT=g_codes[b, a, t].bitcast(E5M2X4),
-                    lhsT_scale=g_plane[b, a, t],
-                    rhs=am_codes[a][:, half * 2 * SPAN : (half + 1) * 2 * SPAN].bitcast(E2M1X4),
-                    rhs_scale=am_plane[:, a, half * SPAN : (half + 1) * SPAN],
-                    start=(a == 0),
-                    stop=(a == 1),
-                )
-
-        h_rows = {}
-
-        def drain_h(b, half, t, pairs, on_vector=False):
-            if (b, half) not in h_rows:
-                h_rows[b, half] = sbuf("h_rows%d%d" % (b, half), [P, PACK, SPAN], BF16)
-            cols = slice(pairs.start * 2 * P, pairs.stop * 2 * P)
-            dst = h_rows[b, half][:, t, cols]
-            src = h_acc[b, half, t][:, cols]
-            if on_vector:
-                nc.vector.tensor_copy(out=dst, in_=src)
-            else:
-                nc.scalar.copy(out=dst, in_=src)
-
-        h_grouped = {}
-
-        def grouped_part(b, half, pair, shared=False):
-            if (b, half, pair) not in h_grouped:
-                tag = "shared" if shared else "h_grouped%d%d%d" % (b, half, pair)
-                h_grouped[b, half, pair] = sb.tile([P, 2 * SPAN], BF16, name="h_grouped", tag=tag, align_bytes=256)
-            return h_grouped[b, half, pair][:]
-
-        def interleave_h(b, half, pair, on_vector, groups=slice(0, P // 2)):
-            dst = grouped_part(b, half, pair).rearrange("p (u c i t) -> p c t i u", u=2, i=2, t=PACK)
-            src = h_rows[b, half][:, :, pair * 2 * P : (pair + 1) * 2 * P].rearrange("p t (c i u) -> p c t i u", i=2, u=2)
-            if on_vector:
-                nc.vector.tensor_copy(out=dst[:, groups], in_=src[:, groups])
-            else:
-                nc.scalar.copy(out=dst[:, groups], in_=src[:, groups])
-
-        h_codes = {}
-        h_plane = {}
-
-        def quantize_h(b, half, pair):
-            codes = sbuf("h_codes%d%d%d" % (b, half, pair), [P, 2 * P], U32)
-            plane = sbuf("h_plane%d%d%d" % (b, half, pair), [P, 2 * P], U8)
-            nc.vector.quantize_mx(out=codes[:].bitcast(E4M3X4), scales=plane[:], in_=grouped_part(b, half, pair))
-            for u in range(2):
-                h_codes[b, PACK * half + 2 * pair + u] = codes[:, u * P : (u + 1) * P]
-                h_plane[b, PACK * half + 2 * pair + u] = plane[:, u * P : (u + 1) * P]
-
-        tile_rows = {}
-        tile_grouped = {}
-
-        def drain_tile(u, t, on_vector):
-            if u not in tile_rows:
-                tile_rows[u] = sbuf("tile_rows%d" % u, [P, PACK, P], BF16)
-            src = h_acc[1, 0, t][:, : 2 * P].rearrange("p (q u) -> p u q", u=2)[:, u, :]
-            if on_vector:
-                nc.vector.tensor_copy(out=tile_rows[u][:, t, :], in_=src)
-            else:
-                nc.scalar.copy(out=tile_rows[u][:, t, :], in_=src)
-
-        def interleave_tile(u):
-            part = grouped_part(1, 0, 0)[:, u * SPAN : (u + 1) * SPAN]
-            nc.vector.tensor_copy(
-                out=part.rearrange("p (c i t) -> p c t i", i=4, t=PACK),
-                in_=tile_rows[u][:].rearrange("p t (c i) -> p c t i", i=4),
-            )
-
-        def quantize_tile(u):
-            codes = sbuf("tile_codes%d" % u, [P, P], U32)
-            plane = sbuf("tile_plane%d" % u, [P, P], U8)
-            nc.vector.quantize_mx(
-                out=codes[:].bitcast(E4M3X4), scales=plane[:], in_=grouped_part(1, 0, 0)[:, u * SPAN : (u + 1) * SPAN]
-            )
-            h_codes[1, u] = codes[:]
-            h_plane[1, u] = plane[:]
-
-        y_acc = {}
-
-        def multiply_y(tile, side, b):
-            if b == 0:
-                y_acc[tile, side] = bank(2 * (tile % Y_BANK_PAIRS) + side)
-            nc.tensor.matmul_mx(
-                out=y_acc[tile, side][:],
-                lhsT=h_codes[b, tile].bitcast(E4M3X4),
-                lhsT_scale=h_plane[b, tile],
-                rhs=bm_codes[:, b, side * 2 * SPAN : (side + 1) * 2 * SPAN].bitcast(E2M1X4),
-                rhs_scale=bm_plane[:, b, side * SPAN : (side + 1) * SPAN],
-                start=(b == 0),
-                stop=(b == 1),
-            )
-
-        def multiply_tile(tile):
-            for side in range(2):
-                for b in range(2):
-                    multiply_y(tile, side, b)
-
-        result = {}
-
-        def finish_bank(tile, side):
-            pair, u = divmod(tile, 2)
-            if pair not in result:
-                result[pair] = sbuf("result%d" % pair, [P, 2 * N], F32)
-            cols = slice(u * N + side * SPAN, u * N + (side + 1) * SPAN)
-            nc.vector.scalar_tensor_tensor(
-                out=result[pair][:, cols],
-                in0=mom_sb[pair][:, cols],
-                scalar=DECAY,
-                in1=y_acc[tile, side][:],
-                op0=mybir.AluOpType.mult,
-                op1=mybir.AluOpType.add,
-            )
-
-        def store(pair, cols):
-            rows = out[pair * 2 * P : (pair + 1) * 2 * P, :].rearrange("(q u) n -> q (u n)", u=2)
-            nc.sync.dma_start(out=rows[:, cols], in_=result[pair][:, cols])
-
-        def finish(tile):
-            finish_bank(tile, 0)
-            finish_bank(tile, 1)
-
-        def store_tile(tile):
-            pair, u = divmod(tile, 2)
-            store(pair, slice(u * N, (u + 1) * N))
-
-        def store_bank(tile, side):
-            pair, u = divmod(tile, 2)
-            store(pair, slice(u * N + side * SPAN, u * N + (side + 1) * SPAN))
-
-        both = range(2)
-        low = range(0, 1)
-        high = range(1, 2)
+        load_mom(range(0, 4))
+        load_mom(range(4, 6))
+        load_mom(range(6, 8))
 
         interleave_g(0, 0, 20)
-        quantize_g(0, 0, 2)
-        multiply_h(0, 0, 0)
-        multiply_h(0, 0, 1, range(3))
+        quantize_g(0, 0)
+        for slots in (range(0, 2), range(2, 4)):
+            for strip in range(BANKS):
+                for t in slots:
+                    pass_h(0, 0, strip, t)
         interleave_g(0, 1, 20)
-        quantize_g(0, 1, 2)
-        multiply_h(0, 1, 0)
-        multiply_h(0, 0, 1, range(3, 4))
-        multiply_h(0, 1, 1)
-        for t in range(PACK):
-            drain_h(0, 0, t, both)
+        quantize_g(0, 1)
+        multiply_h(0, 1, range(BANKS))
+        drain_h(0, 0, True)
+        for strip in range(1, 6):
+            drain_h(0, strip)
         interleave_g(1, 0, P // 2)
-        quantize_g(1, 0, 2)
-        drain_h(0, 1, 0, both)
-        multiply_h(1, 0, 0)
-        interleave_h(0, 0, 0, True, slice(0, 16))
-        interleave_g(1, 1, 20)
-        quantize_g(1, 1, 2)
-        for t in range(1, 4):
-            drain_h(0, 1, t, both)
-        multiply_h(1, 0, 1, range(1))
-        multiply_h(1, 1, 0)
-        multiply_h(1, 0, 1, range(1, 4))
-        multiply_h(1, 1, 1)
-        interleave_h(0, 0, 0, True, slice(16, 64))
-        interleave_h(0, 0, 1, True)
-        quantize_h(0, 0, 0)
-        for t in range(PACK):
-            drain_tile(0, t, t == 3)
-        for t in range(PACK):
-            drain_tile(1, t, t == 3)
-        drain_h(1, 0, 0, high)
-        drain_h(1, 0, 1, high)
-        interleave_tile(0)
-        interleave_tile(1)
-        quantize_tile(0)
-        quantize_tile(1)
-        drain_h(1, 0, 2, high)
-        drain_h(1, 0, 3, high)
-        quantize_h(0, 0, 1)
-        multiply_tile(0)
-        multiply_tile(1)
-        drain_h(1, 1, 0, low)
-        interleave_h(1, 0, 1, False)
-        interleave_h(0, 1, 0, True)
-        drain_h(1, 1, 0, high)
-        drain_h(1, 1, 1, both)
-        drain_h(1, 1, 2, low)
-        drain_h(1, 1, 3, low)
-        drain_h(1, 1, 2, high)
+        quantize_g(1, 0)
+        multiply_h(1, 0, range(6))
+        quantize_h(0, range(0, 4))
+        interleave_g(1, 1, 12)
+        quantize_g(1, 1)
+        drain_h(0, 6)
+        drain_h(0, 7)
+        multiply_h(1, 1, range(6))
+        multiply_h(1, 0, range(6, 7))
+        multiply_h(1, 1, range(6, 7))
+        for strip in range(ROWS):
+            drain_h(1, strip, strip % 2 == 1)
+        quantize_h(1, range(0, 2))
+        quantize_h(1, range(2, 4))
+        quantize_h(0, range(4, 8))
+        multiply_y(0)
+        multiply_h(1, 0, range(7, 8))
+        multiply_h(1, 1, range(7, 8))
+        for strip in range(ROWS, BANKS):
+            drain_h(1, strip)
+        for tile in range(1, ROWS):
+            multiply_y(tile)
         finish(0)
-        store_tile(0)
-        quantize_h(1, 0, 1)
-        quantize_h(0, 1, 0)
-        multiply_tile(2)
-        multiply_tile(3)
-        interleave_h(1, 1, 0, False)
-        drain_h(1, 1, 3, high)
-        interleave_h(0, 1, 1, False)
-        interleave_h(1, 1, 1, False)
         finish(1)
-        store_tile(1)
-        finish(2)
-        store_tile(2)
-        quantize_h(1, 1, 0)
-
-        multiply_tile(4)
-        multiply_tile(5)
-        finish(3)
-        store_tile(3)
-        finish_bank(4, 0)
-        store_bank(4, 0)
-        quantize_h(0, 1, 1)
-        finish_bank(4, 1)
-        store_bank(4, 1)
-        quantize_h(1, 1, 1)
-        multiply_tile(6)
-        multiply_tile(7)
-        for tile in range(5, 8):
-            for side in range(2):
-                finish_bank(tile, side)
-                store_bank(tile, side)
+        store(range(0, 2))
+        quantize_h(1, range(4, 8))
+        for tile in range(2, 8):
+            if tile + 2 < 8:
+                multiply_y(tile + 2)
+            finish(tile)
+            if tile % 2 == 1:
+                store(range(tile - 1, tile + 1))

@@ -19,7 +19,7 @@ PACK = 4
 SPAN = P * PACK
 BANKS = 8
 DECAY = 0.9
-ROWS = 4
+ROWS = 2
 
 
 def tile_mix_kfac_ema_kernel(tc, g, am_words, am_scales, bm_words, bm_scales, mom, out):
@@ -59,15 +59,15 @@ def tile_mix_kfac_ema_kernel(tc, g, am_words, am_scales, bm_words, bm_scales, mo
             am_codes[a] = sbuf("am_codes%d" % a, [P, 2 * M], U8)
             nc.sync.dma_start(out=am_codes[a][:].bitcast(I32), in_=am_words[a].bitcast(I32))
 
-        def half_rows(matrix, half):
-            return matrix[half * SPAN : (half + 1) * SPAN, :].rearrange("(q w) n -> q (w n)", w=ROWS)
+        def group_rows(matrix, group):
+            return matrix[group * ROWS * P : (group + 1) * ROWS * P, :].rearrange("(q w) n -> q (w n)", w=ROWS)
 
         mom_sb = {}
 
         def load_mom(tiles):
-            half, first = divmod(tiles.start, ROWS)
+            group, first = divmod(tiles.start, ROWS)
             held = sbuf("mom%d" % tiles.start, [P, len(tiles) * N], F32)
-            nc.sync.dma_start(out=held[:], in_=half_rows(mom, half)[:, first * N : (first + len(tiles)) * N])
+            nc.sync.dma_start(out=held[:], in_=group_rows(mom, group)[:, first * N : (first + len(tiles)) * N])
             for tile in tiles:
                 mom_sb[tile] = held[:, (tile - tiles.start) * N : (tile - tiles.start + 1) * N]
 
@@ -117,14 +117,20 @@ def tile_mix_kfac_ema_kernel(tc, g, am_words, am_scales, bm_words, bm_scales, mo
                 for t in range(PACK):
                     pass_h(b, a, strip, t)
 
+        def multiply_by_slot_pair(b, a, strips):
+            for slots in (range(0, 2), range(2, 4)):
+                for strip in strips:
+                    for t in slots:
+                        pass_h(b, a, strip, t)
+
         h_grouped = {}
 
         def drain_h(b, strip, on_vector=False):
-            half, part = divmod(strip, ROWS)
-            if (b, half) not in h_grouped:
-                h_grouped[b, half] = sbuf("h_grouped%d%d" % (b, half), [P, ROWS * SPAN], BF16)
+            group, part = divmod(strip, ROWS)
+            if (b, group) not in h_grouped:
+                h_grouped[b, group] = sbuf("h_grouped%d%d" % (b, group), [P, ROWS * SPAN], BF16)
             width = P // ROWS
-            dst = h_grouped[b, half][:].rearrange("p (w q t) -> p w q t", w=ROWS, t=PACK)[:, :, part * width : (part + 1) * width, :]
+            dst = h_grouped[b, group][:].rearrange("p (w q t) -> p w q t", w=ROWS, t=PACK)[:, :, part * width : (part + 1) * width, :]
             src = h_acc[b, strip][:].rearrange("p (t q w) -> p w q t", t=PACK, w=ROWS)
             if on_vector:
                 nc.vector.tensor_copy(out=dst, in_=src)
@@ -135,13 +141,13 @@ def tile_mix_kfac_ema_kernel(tc, g, am_words, am_scales, bm_words, bm_scales, mo
         h_plane = {}
 
         def quantize_h(b, tiles):
-            half, first = divmod(tiles.start, ROWS)
+            group, first = divmod(tiles.start, ROWS)
             codes = sbuf("h_codes%d%d" % (b, tiles.start), [P, len(tiles) * P], U32)
             plane = sbuf("h_plane%d%d" % (b, tiles.start), [P, len(tiles) * P], U8)
             nc.vector.quantize_mx(
                 out=codes[:].bitcast(E4M3X4),
                 scales=plane[:],
-                in_=h_grouped[b, half][:, first * SPAN : (first + len(tiles)) * SPAN],
+                in_=h_grouped[b, group][:, first * SPAN : (first + len(tiles)) * SPAN],
             )
             for u in range(len(tiles)):
                 h_codes[b, tiles.start + u] = codes[:, u * P : (u + 1) * P]
@@ -149,9 +155,9 @@ def tile_mix_kfac_ema_kernel(tc, g, am_words, am_scales, bm_words, bm_scales, mo
 
         y_acc = {}
 
-        def multiply_y(tile):
+        def multiply_y(tile, bank_pair):
             for side in range(2):
-                y_acc[tile, side] = bank((2 * tile + side) % BANKS)
+                y_acc[tile, side] = bank(2 * bank_pair + side)
                 for b in range(2):
                     nc.tensor.matmul_mx(
                         out=y_acc[tile, side][:],
@@ -166,12 +172,12 @@ def tile_mix_kfac_ema_kernel(tc, g, am_words, am_scales, bm_words, bm_scales, mo
         result = {}
 
         def finish(tile):
-            half, w = divmod(tile, ROWS)
-            if half not in result:
-                result[half] = sbuf("result%d" % half, [P, ROWS * N], F32)
+            group, w = divmod(tile, ROWS)
+            if group not in result:
+                result[group] = sbuf("result%d" % group, [P, ROWS * N], F32)
             for side in range(2):
                 nc.vector.scalar_tensor_tensor(
-                    out=result[half][:, w * N + side * SPAN : w * N + (side + 1) * SPAN],
+                    out=result[group][:, w * N + side * SPAN : w * N + (side + 1) * SPAN],
                     in0=mom_sb[tile][:, side * SPAN : (side + 1) * SPAN],
                     scalar=DECAY,
                     in1=y_acc[tile, side][:],
@@ -180,9 +186,9 @@ def tile_mix_kfac_ema_kernel(tc, g, am_words, am_scales, bm_words, bm_scales, mo
                 )
 
         def store(tiles):
-            half, first = divmod(tiles.start, ROWS)
+            group, first = divmod(tiles.start, ROWS)
             cols = slice(first * N, (first + len(tiles)) * N)
-            nc.sync.dma_start(out=half_rows(out, half)[:, cols], in_=result[half][:, cols])
+            nc.sync.dma_start(out=group_rows(out, group)[:, cols], in_=result[group][:, cols])
 
         load_g(0, 0)
         load_am(0)
@@ -194,16 +200,12 @@ def tile_mix_kfac_ema_kernel(tc, g, am_words, am_scales, bm_words, bm_scales, mo
         bm_codes = sbuf("bm_codes", [P, 2, 2 * N], U8)
         nc.sync.dma_start(out=bm_codes[:].bitcast(I32), in_=bm_words.rearrange("a p c -> p a c").bitcast(I32))
         load_plane(bm_plane, bm_scales)
-        load_mom(range(0, 4))
-        load_mom(range(4, 6))
-        load_mom(range(6, 8))
+        for first in range(0, 8, ROWS):
+            load_mom(range(first, first + ROWS))
 
         interleave_g(0, 0, 20)
         quantize_g(0, 0)
-        for slots in (range(0, 2), range(2, 4)):
-            for strip in range(BANKS):
-                for t in slots:
-                    pass_h(0, 0, strip, t)
+        multiply_by_slot_pair(0, 0, range(BANKS))
         interleave_g(0, 1, 20)
         quantize_g(0, 1)
         multiply_h(0, 1, range(BANKS))
@@ -213,33 +215,38 @@ def tile_mix_kfac_ema_kernel(tc, g, am_words, am_scales, bm_words, bm_scales, mo
         interleave_g(1, 0, P // 2)
         quantize_g(1, 0)
         multiply_h(1, 0, range(6))
-        quantize_h(0, range(0, 4))
-        interleave_g(1, 1, 12)
+        quantize_h(0, range(0, 2))
+        quantize_h(0, range(2, 4))
+        interleave_g(1, 1, 20)
         quantize_g(1, 1)
         drain_h(0, 6)
         drain_h(0, 7)
-        multiply_h(1, 1, range(6))
-        multiply_h(1, 0, range(6, 7))
-        multiply_h(1, 1, range(6, 7))
-        for strip in range(ROWS):
-            drain_h(1, strip, strip % 2 == 1)
+        multiply_by_slot_pair(1, 1, range(6))
+        for strip in range(6, 8):
+            multiply_h(1, 0, range(strip, strip + 1))
+            multiply_h(1, 1, range(strip, strip + 1))
+        quantize_h(0, range(4, 6))
+        drain_h(1, 0)
+        drain_h(1, 1, True)
+        quantize_h(0, range(6, 8))
         quantize_h(1, range(0, 2))
-        quantize_h(1, range(2, 4))
-        quantize_h(0, range(4, 8))
-        multiply_y(0)
-        multiply_h(1, 0, range(7, 8))
-        multiply_h(1, 1, range(7, 8))
-        for strip in range(ROWS, BANKS):
+        for strip in range(2, 8):
             drain_h(1, strip)
-        for tile in range(1, ROWS):
-            multiply_y(tile)
+        quantize_h(1, range(2, 4))
+        for tile in range(4):
+            multiply_y(tile, tile)
         finish(0)
+        quantize_h(1, range(4, 6))
+        multiply_y(4, 0)
         finish(1)
         store(range(0, 2))
-        quantize_h(1, range(4, 8))
-        for tile in range(2, 8):
-            if tile + 2 < 8:
-                multiply_y(tile + 2)
+        quantize_h(1, range(6, 8))
+        multiply_y(5, 1)
+        finish(2)
+        multiply_y(6, 2)
+        finish(3)
+        multiply_y(7, 3)
+        store(range(2, 4))
+        for tile in range(4, 8):
             finish(tile)
-            if tile % 2 == 1:
-                store(range(tile - 1, tile + 1))
+            store(range(tile, tile + 1))

@@ -171,11 +171,11 @@ def tile_mix_kfac_ema_kernel(tc, g, am_words, am_scales, bm_words, bm_scales, mo
 
         result = {}
 
-        def finish(tile):
+        def finish(tile, sides=range(2)):
             group, w = divmod(tile, ROWS)
             if group not in result:
                 result[group] = sbuf("result%d" % group, [P, ROWS * N], F32)
-            for side in range(2):
+            for side in sides:
                 nc.vector.scalar_tensor_tensor(
                     out=result[group][:, w * N + side * SPAN : w * N + (side + 1) * SPAN],
                     in0=mom_sb[tile][:, side * SPAN : (side + 1) * SPAN],
@@ -185,9 +185,9 @@ def tile_mix_kfac_ema_kernel(tc, g, am_words, am_scales, bm_words, bm_scales, mo
                     op1=mybir.AluOpType.add,
                 )
 
-        def store(tiles):
-            group, first = divmod(tiles.start, ROWS)
-            cols = slice(first * N, (first + len(tiles)) * N)
+        def store(banks):
+            group, first = divmod(banks.start, 2 * ROWS)
+            cols = slice(first * SPAN, (first + len(banks)) * SPAN)
             nc.sync.dma_start(out=group_rows(out, group)[:, cols], in_=result[group][:, cols])
 
         load_g(0, 0)
@@ -221,32 +221,38 @@ def tile_mix_kfac_ema_kernel(tc, g, am_words, am_scales, bm_words, bm_scales, mo
         quantize_g(1, 1)
         drain_h(0, 6)
         drain_h(0, 7)
-        multiply_by_slot_pair(1, 1, range(6))
-        for strip in range(6, 8):
-            multiply_h(1, 0, range(strip, strip + 1))
-            multiply_h(1, 1, range(strip, strip + 1))
+        multiply_by_slot_pair(1, 1, range(2))
+        multiply_h(1, 1, range(2, 6))
+        multiply_h(1, 0, range(6, 7))
+        multiply_h(1, 1, range(6, 7))
         quantize_h(0, range(4, 6))
         drain_h(1, 0)
         drain_h(1, 1, True)
         quantize_h(0, range(6, 8))
         quantize_h(1, range(0, 2))
+        multiply_y(0, 0)
+        multiply_h(1, 0, range(7, 8))
+        multiply_h(1, 1, range(7, 8))
         for strip in range(2, 8):
             drain_h(1, strip)
         quantize_h(1, range(2, 4))
-        for tile in range(4):
+        for tile in range(1, 4):
             multiply_y(tile, tile)
         finish(0)
         quantize_h(1, range(4, 6))
         multiply_y(4, 0)
         finish(1)
-        store(range(0, 2))
+        store(range(0, 4))
         quantize_h(1, range(6, 8))
         multiply_y(5, 1)
         finish(2)
         multiply_y(6, 2)
         finish(3)
         multiply_y(7, 3)
-        store(range(2, 4))
-        for tile in range(4, 8):
+        store(range(4, 8))
+        for tile in range(4, 7):
             finish(tile)
-            store(range(tile, tile + 1))
+            store(range(2 * tile, 2 * tile + 2))
+        for side in range(2):
+            finish(7, range(side, side + 1))
+            store(range(14 + side, 15 + side))

@@ -239,20 +239,20 @@ def tile_mix_kfac_ema_kernel(tc, g, am_words, am_scales, bm_words, bm_scales, mo
         for tile in range(1, 4):
             multiply_y(tile, tile)
         finish(0)
+        store(range(0, 2))
         quantize_h(1, range(4, 6))
         multiply_y(4, 0)
         finish(1)
-        store(range(0, 4))
+        store(range(2, 4))
         quantize_h(1, range(6, 8))
         multiply_y(5, 1)
         finish(2)
+        store(range(4, 6))
         multiply_y(6, 2)
         finish(3)
+        store(range(6, 8))
         multiply_y(7, 3)
-        store(range(4, 8))
-        for tile in range(4, 7):
-            finish(tile)
-            store(range(2 * tile, 2 * tile + 2))
-        for side in range(2):
-            finish(7, range(side, side + 1))
-            store(range(14 + side, 15 + side))
+        for tile in range(4, 8):
+            for side in range(2):
+                finish(tile, range(side, side + 1))
+                store(range(2 * tile + side, 2 * tile + side + 1))

@@ -25,6 +25,7 @@ ROWS = 2
 def tile_mix_kfac_ema_kernel(tc, g, am_words, am_scales, bm_words, bm_scales, mom, out):
     nc = tc.nc
     with ExitStack() as ctx:
+        moved = ctx.enter_context(tc.tile_pool(name="moved", bufs=1))
         sb = ctx.enter_context(tc.tile_pool(name="sb", bufs=1))
         psum = ctx.enter_context(tc.psum_pool(name="psum", bufs=1))
         ctx.enter_context(tc.manual_schedule())
@@ -32,11 +33,14 @@ def tile_mix_kfac_ema_kernel(tc, g, am_words, am_scales, bm_words, bm_scales, mo
         def sbuf(name, shape, dtype):
             return sb.tile(shape, dtype, name=name, align_bytes=256)
 
+        def dma_tile(name, shape, dtype):
+            return moved.tile(shape, dtype, name=name, align_bytes=4096)
+
         def bank(index):
             return psum.tile([P, SPAN], F32, name="acc", tag="bank%d" % index)
 
-        am_plane = sbuf("am_plane", [P, 2, M], U8)
-        bm_plane = sbuf("bm_plane", [P, 2, N], U8)
+        am_plane = dma_tile("am_plane", [P, 2, M], U8)
+        bm_plane = dma_tile("bm_plane", [P, 2, N], U8)
         nc.vector.memset(am_plane[:].bitcast(I32), 0)
         nc.vector.memset(bm_plane[:].bitcast(I32), 0)
 
@@ -48,7 +52,7 @@ def tile_mix_kfac_ema_kernel(tc, g, am_words, am_scales, bm_words, bm_scales, mo
         g_raw = {}
 
         def load_g(b, a):
-            held = sbuf("g_raw%d%d" % (b, a), [P, PACK, SPAN], F32)
+            held = dma_tile("g_raw%d%d" % (b, a), [P, PACK, SPAN], F32)
             rows = g[a * SPAN : (a + 1) * SPAN, b * SPAN : (b + 1) * SPAN]
             nc.sync.dma_start(out=held[:], in_=rows.rearrange("(p j) l -> p j l", j=PACK))
             g_raw[b, a] = held[:]
@@ -56,18 +60,19 @@ def tile_mix_kfac_ema_kernel(tc, g, am_words, am_scales, bm_words, bm_scales, mo
         am_codes = {}
 
         def load_am(a):
-            am_codes[a] = sbuf("am_codes%d" % a, [P, 2 * M], U8)
+            am_codes[a] = dma_tile("am_codes%d" % a, [P, 2 * M], U8)
             nc.sync.dma_start(out=am_codes[a][:].bitcast(I32), in_=am_words[a].bitcast(I32))
 
         def group_rows(matrix, group):
             return matrix[group * ROWS * P : (group + 1) * ROWS * P, :].rearrange("(q w) n -> q (w n)", w=ROWS)
 
         mom_sb = {}
+        mom_all = dma_tile("mom", [P, M // P * N], F32)
 
         def load_mom(tiles):
             group, first = divmod(tiles.start, ROWS)
-            held = sbuf("mom%d" % tiles.start, [P, len(tiles) * N], F32)
-            nc.sync.dma_start(out=held[:], in_=group_rows(mom, group)[:, first * N : (first + len(tiles)) * N])
+            held = mom_all[:, tiles.start * N : tiles.stop * N]
+            nc.sync.dma_start(out=held, in_=group_rows(mom, group)[:, first * N : (first + len(tiles)) * N])
             for tile in tiles:
                 mom_sb[tile] = held[:, (tile - tiles.start) * N : (tile - tiles.start + 1) * N]
 
@@ -169,12 +174,11 @@ def tile_mix_kfac_ema_kernel(tc, g, am_words, am_scales, bm_words, bm_scales, mo
                         stop=(b == 1),
                     )
 
-        result = {}
+        result_all = dma_tile("result", [P, M // P * N], F32)
+        result = {group: result_all[:, group * ROWS * N : (group + 1) * ROWS * N] for group in range(M // P // ROWS)}
 
         def finish(tile, sides=range(2)):
             group, w = divmod(tile, ROWS)
-            if group not in result:
-                result[group] = sbuf("result%d" % group, [P, ROWS * N], F32)
             for side in sides:
                 nc.vector.scalar_tensor_tensor(
                     out=result[group][:, w * N + side * SPAN : w * N + (side + 1) * SPAN],
@@ -197,7 +201,7 @@ def tile_mix_kfac_ema_kernel(tc, g, am_words, am_scales, bm_words, bm_scales, mo
         load_am(1)
         load_g(1, 0)
         load_g(1, 1)
-        bm_codes = sbuf("bm_codes", [P, 2, 2 * N], U8)
+        bm_codes = dma_tile("bm_codes", [P, 2, 2 * N], U8)
         nc.sync.dma_start(out=bm_codes[:].bitcast(I32), in_=bm_words.rearrange("a p c -> p a c").bitcast(I32))
         load_plane(bm_plane, bm_scales)
         for first in range(0, 8, ROWS):

from contextlib import ExitStack

import concourse.mybir as mybir

K, L, M, N = 1024, 1024, 1024, 1024
FLOPS = 2 * K * L * M + 2 * L * M * N

F32 = mybir.dt.float32
BF16 = mybir.dt.bfloat16
I32 = mybir.dt.int32
U32 = mybir.dt.uint32
U8 = mybir.dt.uint8
E5M2X4 = mybir.dt.float8_e5m2_x4
E4M3X4 = mybir.dt.float8_e4m3fn_x4
E2M1X4 = mybir.dt.float4_e2m1fn_x4

P = 128
PACK = 4
SPAN = P * PACK
BANKS = 8
DECAY = 0.9
ROWS = 2


def tile_mix_kfac_ema_kernel(tc, g, am_words, am_scales, bm_words, bm_scales, mom, out):
    nc = tc.nc
    with ExitStack() as ctx:
        moved = ctx.enter_context(tc.tile_pool(name="moved", bufs=1))
        sb = ctx.enter_context(tc.tile_pool(name="sb", bufs=1))
        psum = ctx.enter_context(tc.psum_pool(name="psum", bufs=1))
        ctx.enter_context(tc.manual_schedule())

        def sbuf(name, shape, dtype):
            return sb.tile(shape, dtype, name=name, align_bytes=256)

        def dma_tile(name, shape, dtype):
            return moved.tile(shape, dtype, name=name, align_bytes=4096)

        def bank(index):
            return psum.tile([P, SPAN], F32, name="acc", tag="bank%d" % index)

        am_plane = dma_tile("am_plane", [P, 2, M], U8)
        bm_plane = dma_tile("bm_plane", [P, 2, N], U8)
        nc.vector.memset(am_plane[:].bitcast(I32), 0)
        nc.vector.memset(bm_plane[:].bitcast(I32), 0)

        def load_plane(plane, scales):
            rows = scales.rearrange("a (quad r) c -> r quad a c", r=4)
            for r in range(4):
                nc.sync.dma_start(out=plane[r:P:32, :, :].bitcast(I32), in_=rows[r].bitcast(I32))

        g_raw = {}

        def load_g(b, a):
            held = dma_tile("g_raw%d%d" % (b, a), [P, PACK, SPAN], F32)
            rows = g[a * SPAN : (a + 1) * SPAN, b * SPAN : (b + 1) * SPAN]
            nc.sync.dma_start(out=held[:], in_=rows.rearrange("(p j) l -> p j l", j=PACK))
            g_raw[b, a] = held[:]

        am_codes = {}

        def load_am(a):
            am_codes[a] = dma_tile("am_codes%d" % a, [P, 2 * M], U8)
            nc.sync.dma_start(out=am_codes[a][:].bitcast(I32), in_=am_words[a].bitcast(I32))

        def group_rows(matrix, group):
            return matrix[group * ROWS * P : (group + 1) * ROWS * P, :].rearrange("(q w) n -> q (w n)", w=ROWS)

        mom_sb = {}
        mom_all = dma_tile("mom", [P, M // P * N], F32)

        def load_mom(tiles):
            group, first = divmod(tiles.start, ROWS)
            held = mom_all[:, tiles.start * N : tiles.stop * N]
            nc.sync.dma_start(out=held, in_=group_rows(mom, group)[:, first * N : (first + len(tiles)) * N])
            for tile in tiles:
                mom_sb[tile] = held[:, (tile - tiles.start) * N : (tile - tiles.start + 1) * N]

        g_codes = {}
        g_plane = {}
        g_grouped = {}

        def interleave_g(b, a, vector_share):
            g_grouped[b, a] = sbuf("g_grouped%d%d" % (b, a), [P, PACK * SPAN], BF16)
            src = g_raw[b, a].rearrange("p j (c e h t) -> p h c j e t", e=2, h=2, t=2)
            dst = g_grouped[b, a][:].rearrange("p (h t c e j) -> p h c j e t", h=2, t=2, e=2, j=PACK)
            nc.vector.tensor_copy(out=dst[:, 0], in_=src[:, 0])
            nc.vector.tensor_copy(out=dst[:, 1, :vector_share], in_=src[:, 1, :vector_share])
            if vector_share < P // 2:
                nc.scalar.copy(out=dst[:, 1, vector_share:], in_=src[:, 1, vector_share:])

        def quantize_g(b, a):
            for first in range(0, PACK, 2):
                codes = sbuf("g_codes%d%d%d" % (b, a, first), [P, 2 * P], U32)
                plane = sbuf("g_plane%d%d%d" % (b, a, first), [P, 2 * P], U8)
                nc.vector.quantize_mx(
                    out=codes[:].bitcast(E5M2X4),
                    scales=plane[:],
                    in_=g_grouped[b, a][:, first * SPAN : (first + 2) * SPAN],
                )
                for u in range(2):
                    g_codes[b, a, first + u] = codes[:, u * P : (u + 1) * P]
                    g_plane[b, a, first + u] = plane[:, u * P : (u + 1) * P]

        h_acc = {}

        def pass_h(b, a, strip, t):
            if a == 0 and t == 0:
                h_acc[b, strip] = bank(strip)
            nc.tensor.matmul_mx(
                out=h_acc[b, strip][:, t * P : (t + 1) * P],
                lhsT=g_codes[b, a, t].bitcast(E5M2X4),
                lhsT_scale=g_plane[b, a, t],
                rhs=am_codes[a][:, strip * 2 * P : (strip + 1) * 2 * P].bitcast(E2M1X4),
                rhs_scale=am_plane[:, a, strip * P : (strip + 1) * P],
                start=(a == 0 and t == 0),
                stop=(a == 1 and t == PACK - 1),
            )

        def multiply_h(b, a, strips):
            for strip in strips:
                for t in range(PACK):
                    pass_h(b, a, strip, t)

        def multiply_by_slot_pair(b, a, strips):
            for slots in (range(0, 2), range(2, 4)):
                for strip in strips:
                    for t in slots:
                        pass_h(b, a, strip, t)

        h_grouped = {}

        def drain_h(b, strip, on_vector=False):
            group, part = divmod(strip, ROWS)
            if (b, group) not in h_grouped:
                h_grouped[b, group] = sbuf("h_grouped%d%d" % (b, group), [P, ROWS * SPAN], BF16)
            width = P // ROWS
            dst = h_grouped[b, group][:].rearrange("p (w q t) -> p w q t", w=ROWS, t=PACK)[:, :, part * width : (part + 1) * width, :]
            src = h_acc[b, strip][:].rearrange("p (t q w) -> p w q t", t=PACK, w=ROWS)
            if on_vector:
                nc.vector.tensor_copy(out=dst, in_=src)
            else:
                nc.scalar.copy(out=dst, in_=src)

        h_codes = {}
        h_plane = {}

        def quantize_h(b, tiles):
            group, first = divmod(tiles.start, ROWS)
            codes = sbuf("h_codes%d%d" % (b, tiles.start), [P, len(tiles) * P], U32)
            plane = sbuf("h_plane%d%d" % (b, tiles.start), [P, len(tiles) * P], U8)
            nc.vector.quantize_mx(
                out=codes[:].bitcast(E4M3X4),
                scales=plane[:],
                in_=h_grouped[b, group][:, first * SPAN : (first + len(tiles)) * SPAN],
            )
            for u in range(len(tiles)):
                h_codes[b, tiles.start + u] = codes[:, u * P : (u + 1) * P]
                h_plane[b, tiles.start + u] = plane[:, u * P : (u + 1) * P]

        y_acc = {}

        def multiply_y(tile, bank_pair):
            for side in range(2):
                y_acc[tile, side] = bank(2 * bank_pair + side)
                for b in range(2):
                    nc.tensor.matmul_mx(
                        out=y_acc[tile, side][:],
                        lhsT=h_codes[b, tile].bitcast(E4M3X4),
                        lhsT_scale=h_plane[b, tile],
                        rhs=bm_codes[:, b, side * 2 * SPAN : (side + 1) * 2 * SPAN].bitcast(E2M1X4),
                        rhs_scale=bm_plane[:, b, side * SPAN : (side + 1) * SPAN],
                        start=(b == 0),
                        stop=(b == 1),
                    )

        result_all = dma_tile("result", [P, M // P * N], F32)
        result = {group: result_all[:, group * ROWS * N : (group + 1) * ROWS * N] for group in range(M // P // ROWS)}

        def finish(tile, sides=range(2)):
            group, w = divmod(tile, ROWS)
            for side in sides:
                nc.vector.scalar_tensor_tensor(
                    out=result[group][:, w * N + side * SPAN : w * N + (side + 1) * SPAN],
                    in0=mom_sb[tile][:, side * SPAN : (side + 1) * SPAN],
                    scalar=DECAY,
                    in1=y_acc[tile, side][:],
                    op0=mybir.AluOpType.mult,
                    op1=mybir.AluOpType.add,
                )

        def store(banks):
            group, first = divmod(banks.start, 2 * ROWS)
            cols = slice(first * SPAN, (first + len(banks)) * SPAN)
            nc.sync.dma_start(out=group_rows(out, group)[:, cols], in_=result[group][:, cols])

        load_g(0, 0)
        load_am(0)
        load_plane(am_plane, am_scales)
        load_g(0, 1)
        load_am(1)
        load_g(1, 0)
        load_g(1, 1)
        bm_codes = dma_tile("bm_codes", [P, 2, 2 * N], U8)
        nc.sync.dma_start(out=bm_codes[:].bitcast(I32), in_=bm_words.rearrange("a p c -> p a c").bitcast(I32))
        load_plane(bm_plane, bm_scales)
        for first in range(0, 8, ROWS):
            load_mom(range(first, first + ROWS))

        interleave_g(0, 0, 20)
        quantize_g(0, 0)
        multiply_by_slot_pair(0, 0, range(BANKS))
        interleave_g(0, 1, 20)
        quantize_g(0, 1)
        multiply_h(0, 1, range(BANKS))
        drain_h(0, 0, True)
        for strip in range(1, 6):
            drain_h(0, strip)
        interleave_g(1, 0, P // 2)
        quantize_g(1, 0)
        multiply_h(1, 0, range(6))
        quantize_h(0, range(0, 2))
        quantize_h(0, range(2, 4))
        interleave_g(1, 1, 20)
        quantize_g(1, 1)
        drain_h(0, 6)
        drain_h(0, 7)
        multiply_by_slot_pair(1, 1, range(2))
        multiply_h(1, 1, range(2, 6))
        multiply_h(1, 0, range(6, 7))
        multiply_h(1, 1, range(6, 7))
        quantize_h(0, range(4, 6))
        drain_h(1, 0)
        drain_h(1, 1, True)
        quantize_h(0, range(6, 8))
        quantize_h(1, range(0, 2))
        multiply_y(0, 0)
        multiply_h(1, 0, range(7, 8))
        multiply_h(1, 1, range(7, 8))
        for strip in range(2, 8):
            drain_h(1, strip)
        quantize_h(1, range(2, 4))
        for tile in range(1, 4):
            multiply_y(tile, tile)
        finish(0)
        store(range(0, 2))
        quantize_h(1, range(4, 6))
        multiply_y(4, 0)
        finish(1)
        store(range(2, 4))
        quantize_h(1, range(6, 8))
        multiply_y(5, 1)
        finish(2)
        store(range(4, 6))
        multiply_y(6, 2)
        finish(3)
        store(range(6, 8))
        multiply_y(7, 3)
        for tile in range(4, 8):
            for side in range(2):
                finish(tile, range(side, side + 1))
                store(range(2 * tile + side, 2 * tile + side + 1))
